import numpy as np
import ml_dtypes


def mxq(x, axis, fmt="e4m3"):
    dtype, down = {"e4m3": (ml_dtypes.float8_e4m3fn, 7), "e5m2": (ml_dtypes.float8_e5m2, 14)}[fmt]
    v = np.moveaxis(np.asarray(x, np.float32).astype(ml_dtypes.bfloat16).astype(np.float64), axis, -1)
    blocks = v.reshape(v.shape[:-1] + (-1, 32))
    amax = np.abs(blocks).max(-1, keepdims=True)
    byte = np.maximum(np.where(amax > 0, np.frexp(amax)[1] - 1 + 127, 0) - down, 1)
    scale = np.exp2(byte - 127.0)
    codes = (blocks / scale).astype(np.float32).astype(dtype).astype(np.float64)
    return np.moveaxis((codes * scale).reshape(v.shape), -1, axis)


WIDE = False


def mx_kscale(k):
    if not WIDE:
        return np.ones(k)
    levels = np.array([24, -24, 12, -12, 0])
    if k % 512:
        return np.exp2(np.random.permutation(np.resize(levels, k // 32))).repeat(32)
    a = np.empty((k // 512, 16))
    for p in range(k // 512):
        a[p, :8] = np.random.permutation(np.resize(levels, 8))
        for g in range(8):
            far = levels[np.abs(levels - a[p, g]) >= 10]
            a[p, g + 8] = far[np.random.randint(len(far))]
    return np.exp2(a.ravel()).repeat(32)


def f64(x):
    return np.asarray(x).astype(np.float64)


def striped(idx):
    return np.tile(idx.reshape(-1, 16).T, (8, 1)).astype(np.uint16)


def unstriped(offs):
    return offs[:16].T.reshape(-1).astype(np.int64)


E2M1 = np.array([0.0, 0.5, 1.0, 1.5, 2.0, 3.0, 4.0, 6.0, -0.0, -0.5, -1.0, -1.5, -2.0, -3.0, -4.0, -6.0])


def pack_weight(w, fmt):
    k, n = w.shape
    w = f64(np.asarray(w, np.float32).astype(ml_dtypes.bfloat16)).reshape(k // 32, 32, n)
    amax = np.abs(w).max(1)
    if fmt == "e4m3":
        byte = np.frexp(amax)[1] - 1 + 127 - 7
    else:
        mant, ex = np.frexp(amax / 6.0)
        byte = np.where(mant > 0.5, ex, ex - 1) + 127
    byte = np.clip(np.where(amax > 0, byte, 1), 1, 254)
    scaled = (w * np.exp2(127.0 - byte)[:, None, :]).reshape(k, n).astype(np.float32)
    by_word = np.ascontiguousarray(scaled.reshape(k // 512, 128, 4, n).transpose(0, 1, 3, 2))
    if fmt == "e4m3":
        words = by_word.astype(ml_dtypes.float8_e4m3fn).view(np.uint8)
    else:
        c = by_word.astype(ml_dtypes.float4_e2m1fn).view(np.uint8) & 0xF
        words = (c[..., 0::2] | (c[..., 1::2] << 4)).reshape(k // 512, 128, 2 * n)
    return np.ascontiguousarray(words), np.ascontiguousarray(byte.astype(np.uint8).reshape(k // 512, 16, n))


def unpack_weight(words, scales, fmt):
    g, _, n = scales.shape
    words = np.ascontiguousarray(words).reshape(g, 128, n, -1)
    if fmt == "e4m3":
        vals = words.view(ml_dtypes.float8_e4m3fn).astype(np.float64)
    else:
        nib = np.empty((g, 128, n, 4), np.uint8)
        nib[..., 0::2] = words & 0xF
        nib[..., 1::2] = words >> 4
        vals = E2M1[nib]
    vals = vals * np.repeat(np.exp2(scales.astype(np.float64) - 127.0), 8, axis=1)[..., None]
    return vals.transpose(0, 1, 3, 2).reshape(g * 512, n)


K, R, N, T, J = 512, 1024, 256, 4096, 1024


def setup_inputs():
    n = np.random.standard_normal
    s = mx_kscale(K)[:, None]
    u = mx_kscale(R)[:, None]
    p_tab = pack_weight(n((K, T)) * s, "e4m3")
    p_w0 = pack_weight(n((K, R)) / np.sqrt(3 * K) / s * u.T, "e2m1")
    p_w1 = pack_weight(n((K, R)) / np.sqrt(3 * K) / s * u.T, "e2m1")
    p_w2 = pack_weight(n((K, R)) / np.sqrt(3 * K) / s * u.T, "e2m1")
    p_wd = pack_weight(n((R, N)) / np.sqrt(R) / u, "e4m3")
    return {
        "tab_words": p_tab[0],
        "tab_scales": p_tab[1],
        "w0_words": p_w0[0],
        "w0_scales": p_w0[1],
        "w1_words": p_w1[0],
        "w1_scales": p_w1[1],
        "w2_words": p_w2[0],
        "w2_scales": p_w2[1],
        "wd_words": p_wd[0],
        "wd_scales": p_wd[1],
        "res": (n((N, J))).astype(np.float32),
        "offs": striped(np.concatenate([np.random.permutation(T)[:J] for _ in range(3)])),
    }


def reference(tab_words, tab_scales, w0_words, w0_scales, w1_words, w1_scales, w2_words, w2_scales, wd_words, wd_scales, res, offs):
    idx = unstriped(offs).reshape(3, J)
    tab_ = unpack_weight(tab_words, tab_scales, "e4m3")[:, idx]
    w0_ = unpack_weight(w0_words, w0_scales, "e2m1")
    w1_ = unpack_weight(w1_words, w1_scales, "e2m1")
    w2_ = unpack_weight(w2_words, w2_scales, "e2m1")
    a = w0_.T @ tab_[:, 0] + w1_.T @ tab_[:, 1] + w2_.T @ tab_[:, 2]
    h = np.maximum(a, 0.0)
    h_ = mxq(h, 0, "e4m3")
    wd_ = unpack_weight(wd_words, wd_scales, "e4m3")
    y = wd_.T @ h_
    return f64(res) + y

@@ -1,0 +1,195 @@
+from contextlib import ExitStack
+
+import concourse.mybir as mybir
+from concourse.masks import make_identity
+
+K, R, N, T, J = 512, 1024, 256, 4096, 1024
+FLOPS = 2 * (3 * K * R * J + R * N * J)
+
+F32 = mybir.dt.float32
+BF16 = mybir.dt.bfloat16
+I32 = mybir.dt.int32
+U32 = mybir.dt.uint32
+U16 = mybir.dt.uint16
+U8 = mybir.dt.uint8
+FP8X4 = mybir.dt.float8_e4m3fn_x4
+FP4X4 = mybir.dt.float4_e2m1fn_x4
+RELU = mybir.ActivationFunctionType.Relu
+ADD = mybir.AluOpType.add
+
+P = 128
+LISTS = 3
+GATHER = 512
+BANK = 512
+R_PASSES = R // 512
+N_TILES = N // P
+UNITS = [(0, 1), (2, 3), (4, 5), (6,), (7,)]
+TABLE_HEAD = 1024
+
+
+def tile_list_rvq_relu_res_kernel(
+    tc, tab_words, tab_scales, w0_words, w0_scales, w1_words, w1_scales, w2_words, w2_scales,
+    wd_words, wd_scales, res, offs, out,
+):
+    nc = tc.nc
+    w_words_hbm = [w0_words, w1_words, w2_words]
+    w_scales_hbm = [w0_scales, w1_scales, w2_scales]
+
+    with ExitStack() as ctx:
+        keep = ctx.enter_context(tc.tile_pool(name="keep", bufs=1))
+        a_psum = ctx.enter_context(tc.psum_pool(name="a_psum", bufs=5))
+        t_psum = ctx.enter_context(tc.psum_pool(name="t_psum", bufs=2))
+        y_psum = ctx.enter_context(tc.psum_pool(name="y_psum", bufs=1))
+
+        offsets = keep.tile([P, LISTS * J // 16], U16, name="offsets")
+        table = keep.tile([P, T], I32, name="table", align_bytes=64)
+        table_scales = keep.tile([P, T // 4], I32, name="table_scales", align_bytes=64)
+        w_words = [keep.tile([P, 2 * R], U8, name="w_words%d" % g, align_bytes=64) for g in range(LISTS)]
+        w_scales = keep.tile([P, LISTS, R // 4], I32, name="w_scales", align_bytes=64)
+        wd = keep.tile([P, R_PASSES, N], I32, name="wd", align_bytes=64)
+        wd_sc = keep.tile([P, R_PASSES, N // 4], I32, name="wd_sc", align_bytes=64)
+        res_sb = keep.tile([P, N_TILES, J], F32, name="res_sb")
+        out_sb = keep.tile([P, N_TILES, J], F32, name="out_sb")
+        identity = keep.tile([P, P], F32, name="identity")
+
+        nc.vector.memset(table_scales[:], 0)
+        nc.vector.memset(w_scales[:], 0)
+        nc.vector.memset(wd_sc[:], 0)
+        make_identity(nc, identity[:])
+
+        def load_scale_rows(plane, rows):
+            for q in range(4):
+                nc.sync.dma_start(out=plane[32 * q : 32 * q + 4], in_=rows[4 * q : 4 * q + 4])
+
+        def load_weight(g):
+            nc.sync.dma_start(out=w_words[g][:].bitcast(I32), in_=w_words_hbm[g][0].bitcast(I32))
+
+        table_hbm = tab_words[0].rearrange("p t i -> p (t i)").bitcast(I32)
+        nc.sync.dma_start(offsets[:], offs)
+        nc.sync.dma_start(out=table[:, :TABLE_HEAD], in_=table_hbm[:, :TABLE_HEAD])
+        load_scale_rows(table_scales, tab_scales[0].bitcast(I32))
+        nc.sync.dma_start(out=table[:, TABLE_HEAD:], in_=table_hbm[:, TABLE_HEAD:])
+        for g in range(LISTS):
+            load_scale_rows(w_scales[:, g, :], w_scales_hbm[g][0].bitcast(I32))
+            load_weight(g)
+        load_scale_rows(wd_sc, wd_scales.bitcast(I32).rearrange("a q n -> q a n"))
+        nc.sync.dma_start(
+            out=wd[:], in_=wd_words.rearrange("a p n i -> p a (n i)").bitcast(I32)
+        )
+        nc.sync.dma_start(out=res_sb[:], in_=res.rearrange("(m p) j -> p m j", p=P))
+
+        v_words, v_scales = {}, {}
+
+        def gather(picked, window, g, half):
+            first = (g * J + half * GATHER) // 16
+            nc.vector.tensor_copy(picked[:], window.indirect(offsets[:, first : first + GATHER // 16]))
+
+        def gather_words(half):
+            for g in range(LISTS):
+                picked = keep.tile([P, GATHER], U32, name="v_words%d_%d" % (g, half), align_bytes=64)
+                gather(picked, table[:].bitcast(U32), g, half)
+                v_words[g, half] = picked
+
+        def gather_scales(half):
+            for g in range(LISTS):
+                picked = keep.tile([P, GATHER], U8, name="v_scales%d" % g, align_bytes=64)
+                gather(picked, table_scales[:].bitcast(U8), g, half)
+                v_scales[g, half] = picked
+
+        gather_scales(0)
+        gather_words(0)
+        gather_words(1)
+
+        h_rows = {}
+
+        def first_pass(bank, jt, b, g):
+            half, c0 = divmod(jt * P, GATHER)
+            nc.tensor.matmul_mx(
+                out=bank[:],
+                lhsT=v_words[g, half][:, c0 : c0 + P].bitcast(FP8X4),
+                lhsT_scale=v_scales[g, half][:, c0 : c0 + P],
+                rhs=w_words[g][:, 2 * BANK * b : 2 * BANK * (b + 1)].bitcast(FP4X4),
+                rhs_scale=w_scales[:, g, :].bitcast(U8)[:, BANK * b : BANK * (b + 1)],
+                start=(g == 0),
+                stop=(g == LISTS - 1),
+            )
+
+        def relu_out(bank, jt, b):
+            rows = keep.tile([P, BANK], BF16, name="h_rows%d_%d" % (jt, b), align_bytes=64)
+            nc.scalar.activation(
+                out=rows[:].rearrange("j (u p e) -> j u p e", u=2, e=2),
+                in_=bank[:].rearrange("j (p u e) -> j u p e", u=2, e=2),
+                func=RELU,
+            )
+            h_rows[jt, b] = rows
+
+        def first_layer(unit, by_list):
+            keys = [(jt, b) for jt in unit for b in range(R_PASSES)]
+            if by_list:
+                banks = [a_psum.tile([P, BANK], F32, name="a_bank") for key in keys]
+                for g in range(LISTS):
+                    for bank, (jt, b) in zip(banks, keys):
+                        first_pass(bank, jt, b, g)
+                        if g == LISTS - 1:
+                            relu_out(bank, jt, b)
+            else:
+                for jt, b in keys:
+                    bank = a_psum.tile([P, BANK], F32, name="a_bank")
+                    for g in range(LISTS):
+                        first_pass(bank, jt, b, g)
+                    relu_out(bank, jt, b)
+
+        h_codes, h_scales = {}, {}
+
+        def turn_and_quantise(unit):
+            width = P * len(unit)
+            grouped = keep.tile([P, R_PASSES, width, 2], F32, name="grouped%d" % unit[0], align_bytes=64)
+            for place, jt in enumerate(unit):
+                turned = t_psum.tile([P, R_PASSES, 2, P], F32, name="turned")
+                for b in range(R_PASSES):
+                    words = h_rows[jt, b][:].bitcast(F32)
+                    for u in range(2):
+                        nc.tensor.transpose(turned[:, b, u, :], words[:, P * u : P * (u + 1)], identity[:])
+                dst = grouped[:, :, P * place : P * (place + 1), :]
+                src = turned[:].rearrange("p b u j -> p b j u")
+                if jt % 2 == 1 and jt > 1:
+                    nc.vector.tensor_copy(out=dst, in_=src)
+                else:
+                    nc.scalar.copy(out=dst, in_=src)
+            codes = keep.tile([P, R_PASSES * width], U32, name="h_codes%d" % unit[0], align_bytes=64)
+            scales = keep.tile([P, R_PASSES * width], U8, name="h_scales%d" % unit[0], align_bytes=64)
+            nc.vector.quantize_mx(
+                out=codes[:].bitcast(FP8X4),
+                scales=scales[:],
+                in_=grouped[:].rearrange("p b j u -> p (b j u)").bitcast(BF16),
+            )
+            h_codes[unit], h_scales[unit] = codes, scales
+
+        def second_layer(unit):
+            width = P * len(unit)
+            cols = slice(P * unit[0], P * unit[0] + width)
+            y_bank = y_psum.tile([P, BANK], F32, name="y_bank")
+            y = y_bank[:, : N_TILES * width].rearrange("p (m j) -> p m j", m=N_TILES)
+            for m in range(N_TILES):
+                for b in range(R_PASSES):
+                    nc.tensor.matmul_mx(
+                        out=y[:, m, :],
+                        lhsT=wd[:, b, P * m : P * (m + 1)].bitcast(FP8X4),
+                        lhsT_scale=wd_sc[:, b, :].bitcast(U8)[:, P * m : P * (m + 1)],
+                        rhs=h_codes[unit][:, width * b : width * (b + 1)].bitcast(FP8X4),
+                        rhs_scale=h_scales[unit][:, width * b : width * (b + 1)],
+                        start=(b == 0),
+                        stop=(b == R_PASSES - 1),
+                    )
+            nc.vector.tensor_tensor(out=out_sb[:, :, cols], in0=y, in1=res_sb[:, :, cols], op=ADD)
+            nc.sync.dma_start(out=out.rearrange("(m p) j -> p m j", p=P)[:, :, cols], in_=out_sb[:, :, cols])
+
+        for step in range(len(UNITS) + 2):
+            if step < len(UNITS):
+                first_layer(UNITS[step], by_list=(UNITS[step][0] * P) % GATHER == 0)
+            if step == 1:
+                gather_scales(1)
+            if step >= 2:
+                second_layer(UNITS[step - 2])
+            if 1 <= step <= len(UNITS):
+                turn_and_quantise(UNITS[step - 1])

@@ -23,7 +23,8 @@ GATHER = 512
 BANK = 512
 R_PASSES = R // 512
 N_TILES = N // P
-UNITS = [(0, 1), (2, 3), (4, 5), (6,), (7,)]
+PSUM_BANKS = 8
+WARM_PASSES = 5
 TABLE_HEAD = 1024
 
 
@@ -37,9 +38,14 @@ def tile_list_rvq_relu_res_kernel(
 
     with ExitStack() as ctx:
         keep = ctx.enter_context(tc.tile_pool(name="keep", bufs=1))
-        a_psum = ctx.enter_context(tc.psum_pool(name="a_psum", bufs=5))
-        t_psum = ctx.enter_context(tc.psum_pool(name="t_psum", bufs=2))
-        y_psum = ctx.enter_context(tc.psum_pool(name="y_psum", bufs=1))
+        psum = ctx.enter_context(tc.psum_pool(name="psum", bufs=1))
+        taken = []
+
+        def next_bank():
+            turn = len(taken)
+            index = 5 + turn if turn < 3 else turn % PSUM_BANKS
+            taken.append(index)
+            return psum.tile([P, BANK], F32, name="bank%d" % index)
 
         offsets = keep.tile([P, LISTS * J // 16], U16, name="offsets")
         table = keep.tile([P, T], I32, name="table", align_bytes=64)
@@ -97,6 +103,22 @@ def tile_list_rvq_relu_res_kernel(
                 v_scales[g, half] = picked
 
         gather_scales(0)
+        zeros = keep.tile([P, 4 * BANK], BF16, name="zeros", align_bytes=64)
+        zero_codes = keep.tile([P, BANK], U32, name="zero_codes", align_bytes=64)
+        zero_scales = keep.tile([P, BANK], U8, name="zero_scales", align_bytes=64)
+        nc.vector.memset(zeros[:], 0.0)
+        nc.vector.quantize_mx(out=zero_codes[:].bitcast(FP8X4), scales=zero_scales[:], in_=zeros[:])
+        warm_bank = psum.tile([P, BANK], F32, name="bank0")
+        for warm in range(WARM_PASSES):
+            nc.tensor.matmul_mx(
+                out=warm_bank[:],
+                lhsT=zero_codes[:, :P].bitcast(FP8X4),
+                lhsT_scale=v_scales[0, 0][:, :P],
+                rhs=zero_codes[:].bitcast(FP8X4),
+                rhs_scale=zero_scales[:],
+                start=True,
+                stop=True,
+            )
         gather_words(0)
         gather_words(1)
 
@@ -126,7 +148,7 @@ def tile_list_rvq_relu_res_kernel(
         def first_layer(unit, by_list):
             keys = [(jt, b) for jt in unit for b in range(R_PASSES)]
             if by_list:
-                banks = [a_psum.tile([P, BANK], F32, name="a_bank") for key in keys]
+                banks = [next_bank() for key in keys]
                 for g in range(LISTS):
                     for bank, (jt, b) in zip(banks, keys):
                         first_pass(bank, jt, b, g)
@@ -134,7 +156,7 @@ def tile_list_rvq_relu_res_kernel(
                             relu_out(bank, jt, b)
             else:
                 for jt, b in keys:
-                    bank = a_psum.tile([P, BANK], F32, name="a_bank")
+                    bank = next_bank()
                     for g in range(LISTS):
                         first_pass(bank, jt, b, g)
                     relu_out(bank, jt, b)
@@ -143,53 +165,58 @@ def tile_list_rvq_relu_res_kernel(
 
         def turn_and_quantise(unit):
             width = P * len(unit)
-            grouped = keep.tile([P, R_PASSES, width, 2], F32, name="grouped%d" % unit[0], align_bytes=64)
-            for place, jt in enumerate(unit):
-                turned = t_psum.tile([P, R_PASSES, 2, P], F32, name="turned")
-                for b in range(R_PASSES):
-                    words = h_rows[jt, b][:].bitcast(F32)
-                    for u in range(2):
-                        nc.tensor.transpose(turned[:, b, u, :], words[:, P * u : P * (u + 1)], identity[:])
-                dst = grouped[:, :, P * place : P * (place + 1), :]
-                src = turned[:].rearrange("p b u j -> p b j u")
-                if jt % 2 == 1 and jt > 1:
-                    nc.vector.tensor_copy(out=dst, in_=src)
-                else:
-                    nc.scalar.copy(out=dst, in_=src)
-            codes = keep.tile([P, R_PASSES * width], U32, name="h_codes%d" % unit[0], align_bytes=64)
-            scales = keep.tile([P, R_PASSES * width], U8, name="h_scales%d" % unit[0], align_bytes=64)
-            nc.vector.quantize_mx(
-                out=codes[:].bitcast(FP8X4),
-                scales=scales[:],
-                in_=grouped[:].rearrange("p b j u -> p (b j u)").bitcast(BF16),
-            )
-            h_codes[unit], h_scales[unit] = codes, scales
+            for b in range(R_PASSES):
+                grouped = keep.tile([P, width, 2], F32, name="grouped%d_%d" % (unit[0], b), align_bytes=64)
+                for first in range(0, len(unit), 2):
+                    pair = unit[first : first + 2]
+                    turned = next_bank()[:, : 2 * P * len(pair)].rearrange("p (t u j) -> p t u j", u=2, j=P)
+                    for place, jt in enumerate(pair):
+                        words = h_rows[jt, b][:].bitcast(F32)
+                        for u in range(2):
+                            nc.tensor.transpose(turned[:, place, u, :], words[:, P * u : P * (u + 1)], identity[:])
+                    nc.scalar.copy(
+                        out=grouped[:, P * first : P * (first + len(pair)), :].rearrange("p (t j) u -> p t j u", j=P),
+                        in_=turned.rearrange("p t u j -> p t j u"),
+                    )
+                codes = keep.tile([P, width], U32, name="h_codes%d_%d" % (unit[0], b), align_bytes=64)
+                scales = keep.tile([P, width], U8, name="h_scales%d_%d" % (unit[0], b), align_bytes=64)
+                nc.vector.quantize_mx(
+                    out=codes[:].bitcast(FP8X4),
+                    scales=scales[:],
+                    in_=grouped[:].rearrange("p j u -> p (j u)").bitcast(BF16),
+                )
+                h_codes[unit, b], h_scales[unit, b] = codes, scales
 
         def second_layer(unit):
             width = P * len(unit)
             cols = slice(P * unit[0], P * unit[0] + width)
-            y_bank = y_psum.tile([P, BANK], F32, name="y_bank")
-            y = y_bank[:, : N_TILES * width].rearrange("p (m j) -> p m j", m=N_TILES)
-            for m in range(N_TILES):
-                for b in range(R_PASSES):
+            banks = [next_bank() for m in range(N_TILES)]
+            for b in range(R_PASSES):
+                for m in range(N_TILES):
                     nc.tensor.matmul_mx(
-                        out=y[:, m, :],
+                        out=banks[m][:, :width],
                         lhsT=wd[:, b, P * m : P * (m + 1)].bitcast(FP8X4),
                         lhsT_scale=wd_sc[:, b, :].bitcast(U8)[:, P * m : P * (m + 1)],
-                        rhs=h_codes[unit][:, width * b : width * (b + 1)].bitcast(FP8X4),
-                        rhs_scale=h_scales[unit][:, width * b : width * (b + 1)],
+                        rhs=h_codes[unit, b][:].bitcast(FP8X4),
+                        rhs_scale=h_scales[unit, b][:],
                         start=(b == 0),
                         stop=(b == R_PASSES - 1),
                     )
-            nc.vector.tensor_tensor(out=out_sb[:, :, cols], in0=y, in1=res_sb[:, :, cols], op=ADD)
+            for m in range(N_TILES):
+                nc.vector.tensor_tensor(out=out_sb[:, m, cols], in0=banks[m][:, :width], in1=res_sb[:, m, cols], op=ADD)
             nc.sync.dma_start(out=out.rearrange("(m p) j -> p m j", p=P)[:, :, cols], in_=out_sb[:, :, cols])
 
-        for step in range(len(UNITS) + 2):
-            if step < len(UNITS):
-                first_layer(UNITS[step], by_list=(UNITS[step][0] * P) % GATHER == 0)
-            if step == 1:
-                gather_scales(1)
-            if step >= 2:
-                second_layer(UNITS[step - 2])
-            if 1 <= step <= len(UNITS):
-                turn_and_quantise(UNITS[step - 1])
+        first_layer((0, 1), by_list=True)
+        first_layer((2, 3), by_list=False)
+        gather_scales(1)
+        turn_and_quantise((0, 1, 2, 3))
+        first_layer((4, 5), by_list=True)
+        first_layer((6,), by_list=False)
+        turn_and_quantise((4, 5))
+        first_layer((7,), by_list=False)
+        second_layer((0, 1, 2, 3))
+        turn_and_quantise((6,))
+        turn_and_quantise((7,))
+        second_layer((4, 5))
+        second_layer((6,))
+        second_layer((7,))

@@ -1,7 +1,6 @@
 from contextlib import ExitStack
 
 import concourse.mybir as mybir
-from concourse.masks import make_identity
 
 K, R, N, T, J = 512, 1024, 256, 4096, 1024
 FLOPS = 2 * (3 * K * R * J + R * N * J)
@@ -24,8 +23,8 @@ BANK = 512
 R_PASSES = R // 512
 N_TILES = N // P
 PSUM_BANKS = 8
-WARM_PASSES = 5
-TABLE_HEAD = 1024
+WARM_PASSES = 4
+TABLE_HEAD = 768
 
 
 def tile_list_rvq_relu_res_kernel(
@@ -51,32 +50,39 @@ def tile_list_rvq_relu_res_kernel(
         table = keep.tile([P, T], I32, name="table", align_bytes=64)
         table_scales = keep.tile([P, T // 4], I32, name="table_scales", align_bytes=64)
         w_words = [keep.tile([P, 2 * R], U8, name="w_words%d" % g, align_bytes=64) for g in range(LISTS)]
-        w_scales = keep.tile([P, LISTS, R // 4], I32, name="w_scales", align_bytes=64)
+        w_scales = [keep.tile([P, R // 4], I32, name="w_scales%d" % g, align_bytes=64) for g in range(LISTS)]
         wd = keep.tile([P, R_PASSES, N], I32, name="wd", align_bytes=64)
         wd_sc = keep.tile([P, R_PASSES, N // 4], I32, name="wd_sc", align_bytes=64)
         res_sb = keep.tile([P, N_TILES, J], F32, name="res_sb")
         out_sb = keep.tile([P, N_TILES, J], F32, name="out_sb")
         identity = keep.tile([P, P], F32, name="identity")
 
-        nc.vector.memset(table_scales[:], 0)
-        nc.vector.memset(w_scales[:], 0)
+        nc.gpsimd.memset(table_scales[:, : T // 8], 0)
+        nc.vector.memset(table_scales[:, T // 8 :], 0)
+        for plane in w_scales:
+            nc.vector.memset(plane[:], 0)
         nc.vector.memset(wd_sc[:], 0)
-        make_identity(nc, identity[:])
+        zeros = keep.tile([P, BANK], F32, name="zeros", align_bytes=64)
+        nc.vector.memset(zeros[:], 0.0)
+        nc.gpsimd.affine_select(
+            out=identity[:], in_=zeros[:, :P], compare_op=mybir.AluOpType.not_equal, fill=1.0,
+            base=0, pattern=[[-1, P]], channel_multiplier=1,
+        )
 
         def load_scale_rows(plane, rows):
-            for q in range(4):
-                nc.sync.dma_start(out=plane[32 * q : 32 * q + 4], in_=rows[4 * q : 4 * q + 4])
+            for r in range(4):
+                nc.sync.dma_start(out=plane[r:P:32], in_=rows[r:16:4])
 
         def load_weight(g):
             nc.sync.dma_start(out=w_words[g][:].bitcast(I32), in_=w_words_hbm[g][0].bitcast(I32))
 
         table_hbm = tab_words[0].rearrange("p t i -> p (t i)").bitcast(I32)
-        nc.sync.dma_start(offsets[:], offs)
         nc.sync.dma_start(out=table[:, :TABLE_HEAD], in_=table_hbm[:, :TABLE_HEAD])
+        nc.sync.dma_start(offsets[:], offs)
         load_scale_rows(table_scales, tab_scales[0].bitcast(I32))
         nc.sync.dma_start(out=table[:, TABLE_HEAD:], in_=table_hbm[:, TABLE_HEAD:])
         for g in range(LISTS):
-            load_scale_rows(w_scales[:, g, :], w_scales_hbm[g][0].bitcast(I32))
+            load_scale_rows(w_scales[g], w_scales_hbm[g][0].bitcast(I32))
             load_weight(g)
         load_scale_rows(wd_sc, wd_scales.bitcast(I32).rearrange("a q n -> q a n"))
         nc.sync.dma_start(
@@ -103,17 +109,18 @@ def tile_list_rvq_relu_res_kernel(
                 v_scales[g, half] = picked
 
         gather_scales(0)
-        zeros = keep.tile([P, 4 * BANK], BF16, name="zeros", align_bytes=64)
         zero_codes = keep.tile([P, BANK], U32, name="zero_codes", align_bytes=64)
         zero_scales = keep.tile([P, BANK], U8, name="zero_scales", align_bytes=64)
-        nc.vector.memset(zeros[:], 0.0)
-        nc.vector.quantize_mx(out=zero_codes[:].bitcast(FP8X4), scales=zero_scales[:], in_=zeros[:])
+        for part in (slice(0, BANK // 2), slice(BANK // 2, BANK)):
+            nc.vector.quantize_mx(
+                out=zero_codes[:, part].bitcast(FP8X4), scales=zero_scales[:, part], in_=zeros[:].bitcast(BF16)
+            )
         warm_bank = psum.tile([P, BANK], F32, name="bank0")
         for warm in range(WARM_PASSES):
             nc.tensor.matmul_mx(
                 out=warm_bank[:],
                 lhsT=zero_codes[:, :P].bitcast(FP8X4),
-                lhsT_scale=v_scales[0, 0][:, :P],
+                lhsT_scale=v_scales[1, 0][:, :P],
                 rhs=zero_codes[:].bitcast(FP8X4),
                 rhs_scale=zero_scales[:],
                 start=True,
@@ -131,7 +138,7 @@ def tile_list_rvq_relu_res_kernel(
                 lhsT=v_words[g, half][:, c0 : c0 + P].bitcast(FP8X4),
                 lhsT_scale=v_scales[g, half][:, c0 : c0 + P],
                 rhs=w_words[g][:, 2 * BANK * b : 2 * BANK * (b + 1)].bitcast(FP4X4),
-                rhs_scale=w_scales[:, g, :].bitcast(U8)[:, BANK * b : BANK * (b + 1)],
+                rhs_scale=w_scales[g][:].bitcast(U8)[:, BANK * b : BANK * (b + 1)],
                 start=(g == 0),
                 stop=(g == LISTS - 1),
             )

@@ -81,9 +81,11 @@ def tile_list_rvq_relu_res_kernel(
         nc.sync.dma_start(offsets[:], offs)
         load_scale_rows(table_scales, tab_scales[0].bitcast(I32))
         nc.sync.dma_start(out=table[:, TABLE_HEAD:], in_=table_hbm[:, TABLE_HEAD:])
-        for g in range(LISTS):
-            load_scale_rows(w_scales[g], w_scales_hbm[g][0].bitcast(I32))
+        load_scale_rows(w_scales[0], w_scales_hbm[0][0].bitcast(I32))
+        load_weight(0)
+        for g in range(1, LISTS):
             load_weight(g)
+            load_scale_rows(w_scales[g], w_scales_hbm[g][0].bitcast(I32))
         load_scale_rows(wd_sc, wd_scales.bitcast(I32).rearrange("a q n -> q a n"))
         nc.sync.dma_start(
             out=wd[:], in_=wd_words.rearrange("a p n i -> p a (n i)").bitcast(I32)

@@ -172,29 +172,39 @@ def tile_list_rvq_relu_res_kernel(
 
         h_codes, h_scales = {}, {}
 
-        def turn_and_quantise(unit):
-            width = P * len(unit)
-            for b in range(R_PASSES):
-                grouped = keep.tile([P, width, 2], F32, name="grouped%d_%d" % (unit[0], b), align_bytes=64)
-                for first in range(0, len(unit), 2):
-                    pair = unit[first : first + 2]
-                    turned = next_bank()[:, : 2 * P * len(pair)].rearrange("p (t u j) -> p t u j", u=2, j=P)
-                    for place, jt in enumerate(pair):
-                        words = h_rows[jt, b][:].bitcast(F32)
-                        for u in range(2):
-                            nc.tensor.transpose(turned[:, place, u, :], words[:, P * u : P * (u + 1)], identity[:])
-                    nc.scalar.copy(
-                        out=grouped[:, P * first : P * (first + len(pair)), :].rearrange("p (t j) u -> p t j u", j=P),
-                        in_=turned.rearrange("p t u j -> p t j u"),
-                    )
-                codes = keep.tile([P, width], U32, name="h_codes%d_%d" % (unit[0], b), align_bytes=64)
-                scales = keep.tile([P, width], U8, name="h_scales%d_%d" % (unit[0], b), align_bytes=64)
-                nc.vector.quantize_mx(
-                    out=codes[:].bitcast(FP8X4),
-                    scales=scales[:],
-                    in_=grouped[:].rearrange("p j u -> p (j u)").bitcast(BF16),
+        grouped = {}
+
+        def turn(unit, pair, b):
+            if (unit, b) not in grouped:
+                grouped[unit, b] = keep.tile(
+                    [P, P * len(unit), 2], F32, name="grouped%d_%d" % (unit[0], b), align_bytes=64
                 )
-                h_codes[unit, b], h_scales[unit, b] = codes, scales
+            first = pair[0] - unit[0]
+            turned = next_bank()[:, : 2 * P * len(pair)].rearrange("p (t u j) -> p t u j", u=2, j=P)
+            for place, jt in enumerate(pair):
+                words = h_rows[jt, b][:].bitcast(F32)
+                for u in range(2):
+                    nc.tensor.transpose(turned[:, place, u, :], words[:, P * u : P * (u + 1)], identity[:])
+            nc.scalar.copy(
+                out=grouped[unit, b][:, P * first : P * (first + len(pair)), :].rearrange("p (t j) u -> p t j u", j=P),
+                in_=turned.rearrange("p t u j -> p t j u"),
+            )
+
+        def quantise(unit, b):
+            width = P * len(unit)
+            codes = keep.tile([P, width], U32, name="h_codes%d_%d" % (unit[0], b), align_bytes=64)
+            scales = keep.tile([P, width], U8, name="h_scales%d_%d" % (unit[0], b), align_bytes=64)
+            nc.vector.quantize_mx(
+                out=codes[:].bitcast(FP8X4),
+                scales=scales[:],
+                in_=grouped[unit, b][:].rearrange("p j u -> p (j u)").bitcast(BF16),
+            )
+            h_codes[unit, b], h_scales[unit, b] = codes, scales
+
+        def turn_and_quantise(unit):
+            for b in range(R_PASSES):
+                turn(unit, unit, b)
+                quantise(unit, b)
 
         def second_layer(unit):
             width = P * len(unit)
@@ -218,9 +228,15 @@ def tile_list_rvq_relu_res_kernel(
         first_layer((0, 1), by_list=True)
         first_layer((2, 3), by_list=False)
         gather_scales(1)
-        turn_and_quantise((0, 1, 2, 3))
+        wide = (0, 1, 2, 3)
+        turn(wide, (0, 1), 0)
+        turn(wide, (2, 3), 0)
+        quantise(wide, 0)
+        turn(wide, (0, 1), 1)
         first_layer((4, 5), by_list=True)
         first_layer((6,), by_list=False)
+        turn(wide, (2, 3), 1)
+        quantise(wide, 1)
         turn_and_quantise((4, 5))
         first_layer((7,), by_list=False)
         second_layer((0, 1, 2, 3))

@@ -225,18 +225,18 @@ def tile_list_rvq_relu_res_kernel(
                 nc.vector.tensor_tensor(out=out_sb[:, m, cols], in0=banks[m][:, :width], in1=res_sb[:, m, cols], op=ADD)
             nc.sync.dma_start(out=out.rearrange("(m p) j -> p m j", p=P)[:, :, cols], in_=out_sb[:, :, cols])
 
-        first_layer((0, 1), by_list=True)
-        first_layer((2, 3), by_list=False)
-        gather_scales(1)
         wide = (0, 1, 2, 3)
-        turn(wide, (0, 1), 0)
-        turn(wide, (2, 3), 0)
-        quantise(wide, 0)
-        turn(wide, (0, 1), 1)
+        first_layer((0, 1), by_list=True)
+        first_layer((2,), by_list=False)
+        first_layer((3,), by_list=True)
+        gather_scales(1)
+        for b in range(R_PASSES):
+            turn(wide, (0, 1), b)
         first_layer((4, 5), by_list=True)
+        for b in range(R_PASSES):
+            turn(wide, (2, 3), b)
+            quantise(wide, b)
         first_layer((6,), by_list=False)
-        turn(wide, (2, 3), 1)
-        quantise(wide, 1)
         turn_and_quantise((4, 5))
         first_layer((7,), by_list=False)
         second_layer((0, 1, 2, 3))

@@ -23,7 +23,7 @@ BANK = 512
 R_PASSES = R // 512
 N_TILES = N // P
 PSUM_BANKS = 8
-WARM_PASSES = 4
+WARM_PASSES = 5
 TABLE_HEAD = 768
 
 
@@ -122,7 +122,7 @@ def tile_list_rvq_relu_res_kernel(
             nc.tensor.matmul_mx(
                 out=warm_bank[:],
                 lhsT=zero_codes[:, :P].bitcast(FP8X4),
-                lhsT_scale=v_scales[1, 0][:, :P],
+                lhsT_scale=v_scales[min(warm, 1), 0][:, :P],
                 rhs=zero_codes[:].bitcast(FP8X4),
                 rhs_scale=zero_scales[:],
                 start=True,

@@ -186,8 +186,10 @@ def tile_list_rvq_relu_res_kernel(
                 for u in range(2):
                     nc.tensor.transpose(turned[:, place, u, :], words[:, P * u : P * (u + 1)], identity[:])
             nc.scalar.copy(
-                out=grouped[unit, b][:, P * first : P * (first + len(pair)), :].rearrange("p (t j) u -> p t j u", j=P),
-                in_=turned.rearrange("p t u j -> p t j u"),
+                out=grouped[unit, b][:, P * first : P * (first + len(pair)), :].rearrange(
+                    "p (t c i) u -> p t c u i", c=P // 2, i=2
+                ),
+                in_=turned.rearrange("p t u (c i) -> p t c u i", i=2),
             )
 
         def quantise(unit, b):

@@ -24,7 +24,7 @@ R_PASSES = R // 512
 N_TILES = N // P
 PSUM_BANKS = 8
 WARM_PASSES = 5
-TABLE_HEAD = 768
+TABLE_HEAD = 512
 
 
 def tile_list_rvq_relu_res_kernel(

@@ -18,13 +18,13 @@ ADD = mybir.AluOpType.add
 
 P = 128
 LISTS = 3
-GATHER = 512
+HALF = 512
+QUARTER = 256
 BANK = 512
 R_PASSES = R // 512
 N_TILES = N // P
-PSUM_BANKS = 8
 WARM_PASSES = 5
-TABLE_HEAD = 512
+TABLE_HEAD = 640
 
 
 def tile_list_rvq_relu_res_kernel(
@@ -38,76 +38,106 @@ def tile_list_rvq_relu_res_kernel(
     with ExitStack() as ctx:
         keep = ctx.enter_context(tc.tile_pool(name="keep", bufs=1))
         psum = ctx.enter_context(tc.psum_pool(name="psum", bufs=1))
-        taken = []
 
-        def next_bank():
-            turn = len(taken)
-            index = 5 + turn if turn < 3 else turn % PSUM_BANKS
-            taken.append(index)
+        def bank(index):
             return psum.tile([P, BANK], F32, name="bank%d" % index)
 
         offsets = keep.tile([P, LISTS * J // 16], U16, name="offsets")
         table = keep.tile([P, T], I32, name="table", align_bytes=64)
         table_scales = keep.tile([P, T // 4], I32, name="table_scales", align_bytes=64)
-        w_words = [keep.tile([P, 2 * R], U8, name="w_words%d" % g, align_bytes=64) for g in range(LISTS)]
-        w_scales = [keep.tile([P, R // 4], I32, name="w_scales%d" % g, align_bytes=64) for g in range(LISTS)]
+        staged = keep.tile([P, LISTS * P], I32, name="staged", align_bytes=64)
+        staged_dealt = keep.tile([P, LISTS * P], I32, name="staged_dealt", align_bytes=64)
+        w_scales = keep.tile([P, R_PASSES * LISTS * P], I32, name="w_scales", align_bytes=64)
         wd = keep.tile([P, R_PASSES, N], I32, name="wd", align_bytes=64)
         wd_sc = keep.tile([P, R_PASSES, N // 4], I32, name="wd_sc", align_bytes=64)
         res_sb = keep.tile([P, N_TILES, J], F32, name="res_sb")
         out_sb = keep.tile([P, N_TILES, J], F32, name="out_sb")
-        identity = keep.tile([P, P], F32, name="identity")
 
         nc.gpsimd.memset(table_scales[:, : T // 8], 0)
         nc.vector.memset(table_scales[:, T // 8 :], 0)
-        for plane in w_scales:
-            nc.vector.memset(plane[:], 0)
-        nc.vector.memset(wd_sc[:], 0)
+        nc.vector.memset(staged[32:64, :], 0)
+        nc.vector.memset(staged[64:P, :], 0)
+        nc.gpsimd.memset(w_scales[:], 0)
+        nc.gpsimd.memset(wd_sc[:], 0)
         zeros = keep.tile([P, BANK], F32, name="zeros", align_bytes=64)
         nc.vector.memset(zeros[:], 0.0)
-        nc.gpsimd.affine_select(
-            out=identity[:], in_=zeros[:, :P], compare_op=mybir.AluOpType.not_equal, fill=1.0,
-            base=0, pattern=[[-1, P]], channel_multiplier=1,
+
+        for g in range(LISTS):
+            nc.sync.dma_start(
+                out=staged[0:32, P * g : P * (g + 1)],
+                in_=w_scales_hbm[g][0].bitcast(I32).rearrange("q (b c) -> (q b) c", b=R_PASSES),
+            )
+        nc.gpsimd.tensor_copy(
+            out=staged_dealt[:].bitcast(U8).rearrange("p (g t c i) -> p c g t i", g=LISTS, t=4, i=16),
+            in_=staged[:].bitcast(U8).rearrange("p (g c i t) -> p c g t i", g=LISTS, t=4, i=16),
         )
 
         def load_scale_rows(plane, rows):
             for r in range(4):
                 nc.sync.dma_start(out=plane[r:P:32], in_=rows[r:16:4])
 
-        def load_weight(g):
-            nc.sync.dma_start(out=w_words[g][:].bitcast(I32), in_=w_words_hbm[g][0].bitcast(I32))
+        def carry_scale_rows(b):
+            for r in range(4):
+                nc.sync.dma_start(
+                    out=w_scales[r:P:32, LISTS * P * b : LISTS * P * (b + 1)],
+                    in_=staged_dealt[2 * r + b : 32 : 8, :],
+                )
+
+        w_raw = {}
+
+        def load_weight(g, passes):
+            raw = keep.tile([P, 256 * len(passes)], I32, name="w_raw%d_%d" % (g, passes[0]), align_bytes=64)
+            nc.sync.dma_start(
+                out=raw[:], in_=w_words_hbm[g][0].bitcast(I32)[:, 256 * passes[0] : 256 * (passes[-1] + 1)]
+            )
+            for place, b in enumerate(passes):
+                w_raw[g, b] = raw[:, 256 * place : 256 * (place + 1)]
 
         table_hbm = tab_words[0].rearrange("p t i -> p (t i)").bitcast(I32)
         nc.sync.dma_start(out=table[:, :TABLE_HEAD], in_=table_hbm[:, :TABLE_HEAD])
-        nc.sync.dma_start(offsets[:], offs)
         load_scale_rows(table_scales, tab_scales[0].bitcast(I32))
+        nc.sync.dma_start(offsets[:], offs)
         nc.sync.dma_start(out=table[:, TABLE_HEAD:], in_=table_hbm[:, TABLE_HEAD:])
-        load_scale_rows(w_scales[0], w_scales_hbm[0][0].bitcast(I32))
-        load_weight(0)
-        for g in range(1, LISTS):
-            load_weight(g)
-            load_scale_rows(w_scales[g], w_scales_hbm[g][0].bitcast(I32))
+        load_weight(0, (0,))
+        carry_scale_rows(0)
+        load_weight(1, (0, 1))
+        load_weight(2, (0, 1))
+        load_weight(0, (1,))
+        carry_scale_rows(1)
         load_scale_rows(wd_sc, wd_scales.bitcast(I32).rearrange("a q n -> q a n"))
         nc.sync.dma_start(
             out=wd[:], in_=wd_words.rearrange("a p n i -> p a (n i)").bitcast(I32)
         )
         nc.sync.dma_start(out=res_sb[:], in_=res.rearrange("(m p) j -> p m j", p=P))
 
+        w_dealt = {}
+        for b in range(R_PASSES):
+            for g in range(LISTS):
+                dealt = keep.tile([P, 1024], U8, name="w_dealt%d_%d" % (g, b), align_bytes=64)
+                nc.scalar.copy(
+                    out=dealt[:].bitcast(U16).rearrange("p (t c i) -> p c t i", t=4, i=8),
+                    in_=w_raw[g, b].bitcast(U16).rearrange("p (c i t) -> p c t i", t=4, i=8),
+                )
+                w_dealt[g, b] = dealt
+
         v_words, v_scales = {}, {}
 
-        def gather(picked, window, g, half):
-            first = (g * J + half * GATHER) // 16
-            nc.vector.tensor_copy(picked[:], window.indirect(offsets[:, first : first + GATHER // 16]))
+        def gather(picked, window, g, first, count):
+            column = (g * J + first) // 16
+            nc.vector.tensor_copy(picked, window.indirect(offsets[:, column : column + count // 16]))
 
-        def gather_words(half):
-            for g in range(LISTS):
-                picked = keep.tile([P, GATHER], U32, name="v_words%d_%d" % (g, half), align_bytes=64)
-                gather(picked, table[:].bitcast(U32), g, half)
-                v_words[g, half] = picked
+        def gather_words(picked, g, first_quarter, count):
+            gather(picked, table[:].bitcast(U32), g, first_quarter * QUARTER, count)
+            for c0 in range(0, count, QUARTER):
+                v_words[g, first_quarter + c0 // QUARTER] = picked[:, c0 : c0 + QUARTER]
+
+        def words_tile(name, width):
+            return keep.tile([P, width], U32, name=name, align_bytes=64)
 
         def gather_scales(half):
             for g in range(LISTS):
-                picked = keep.tile([P, GATHER], U8, name="v_scales%d" % g, align_bytes=64)
-                gather(picked, table_scales[:].bitcast(U8), g, half)
+                picked = keep.tile([P, HALF], U8, name="v_scales%d" % g, align_bytes=64)
+                gather(picked[:], table_scales[:].bitcast(U8), g, half * HALF, HALF)
                 v_scales[g, half] = picked
 
         gather_scales(0)
@@ -117,7 +147,7 @@ def tile_list_rvq_relu_res_kernel(
             nc.vector.quantize_mx(
                 out=zero_codes[:, part].bitcast(FP8X4), scales=zero_scales[:, part], in_=zeros[:].bitcast(BF16)
             )
-        warm_bank = psum.tile([P, BANK], F32, name="bank0")
+        warm_bank = bank(0)
         for warm in range(WARM_PASSES):
             nc.tensor.matmul_mx(
                 out=warm_bank[:],
@@ -128,122 +158,162 @@ def tile_list_rvq_relu_res_kernel(
                 start=True,
                 stop=True,
             )
-        gather_words(0)
-        gather_words(1)
+        for g in range(LISTS):
+            for quarter in range(2):
+                gather_words(words_tile("v_words%d_%d" % (g, quarter), QUARTER)[:], g, quarter, QUARTER)
+        for g in range(LISTS):
+            gather_words(words_tile("v_words%d_2" % g, QUARTER)[:], g, 2, QUARTER)
 
-        h_rows = {}
+        pairs, grouped = {}, {}
 
-        def first_pass(bank, jt, b, g):
-            half, c0 = divmod(jt * P, GATHER)
-            nc.tensor.matmul_mx(
-                out=bank[:],
-                lhsT=v_words[g, half][:, c0 : c0 + P].bitcast(FP8X4),
-                lhsT_scale=v_scales[g, half][:, c0 : c0 + P],
-                rhs=w_words[g][:, 2 * BANK * b : 2 * BANK * (b + 1)].bitcast(FP4X4),
-                rhs_scale=w_scales[g][:].bitcast(U8)[:, BANK * b : BANK * (b + 1)],
-                start=(g == 0),
-                stop=(g == LISTS - 1),
-            )
+        def first_passes(acc, quarter, b, u, g):
+            half, c0 = divmod(quarter * QUARTER, HALF)
+            for e in range(2):
+                t = 2 * u + e
+                s0 = 512 * (LISTS * b + g) + P * t
+                nc.tensor.matmul_mx(
+                    out=acc[:, QUARTER * e : QUARTER * (e + 1)],
+                    lhsT=w_dealt[g, b][:, 2 * P * t : 2 * P * (t + 1)].bitcast(FP4X4),
+                    lhsT_scale=w_scales[:].bitcast(U8)[:, s0 : s0 + P],
+                    rhs=v_words[g, quarter].bitcast(FP8X4),
+                    rhs_scale=v_scales[g, half][:, c0 : c0 + QUARTER],
+                    start=(g == 0 and e == 0),
+                    stop=(g == LISTS - 1 and e == 1),
+                )
 
-        def relu_out(bank, jt, b):
-            rows = keep.tile([P, BANK], BF16, name="h_rows%d_%d" % (jt, b), align_bytes=64)
+        def relu_out(acc, quarter, b, u):
+            if u == 0:
+                pairs[quarter, b] = keep.tile(
+                    [P, 2, QUARTER], F32, name="pairs%d_%d" % (quarter, b), align_bytes=64
+                )
             nc.scalar.activation(
-                out=rows[:].rearrange("j (u p e) -> j u p e", u=2, e=2),
-                in_=bank[:].rearrange("j (p u e) -> j u p e", u=2, e=2),
+                out=pairs[quarter, b][:, u, :].bitcast(BF16).rearrange("p (c i e) -> p c e i", i=2, e=2),
+                in_=acc[:].rearrange("p (e c i) -> p c e i", i=2, e=2),
                 func=RELU,
             )
-            h_rows[jt, b] = rows
 
-        def first_layer(unit, by_list):
-            keys = [(jt, b) for jt in unit for b in range(R_PASSES)]
-            if by_list:
-                banks = [next_bank() for key in keys]
+        def weave(quarter, b):
+            half, c0 = divmod(quarter * QUARTER, HALF)
+            if c0 == 0:
+                grouped[half, b] = keep.tile([P, 2 * HALF], F32, name="grouped%d_%d" % (half, b), align_bytes=64)
+            copy = nc.gpsimd.tensor_copy if quarter < 3 else nc.scalar.copy
+            copy(
+                out=grouped[half, b][:, 2 * c0 : 2 * (c0 + QUARTER)].rearrange("p (c i u) -> p c u i", i=4, u=2),
+                in_=pairs[quarter, b][:].rearrange("p u (c i) -> p c u i", i=4),
+            )
+
+        def group_by_list(units, first_bank):
+            keys = [(quarter, b, u) for quarter, b in units for u in range(2)]
+            accs = [bank(first_bank + place) for place in range(len(keys))]
+            for g in range(LISTS):
+                for acc, (quarter, b, u) in zip(accs, keys):
+                    first_passes(acc, quarter, b, u, g)
+                    if g == LISTS - 1:
+                        relu_out(acc, quarter, b, u)
+            for quarter, b in units:
+                weave(quarter, b)
+
+        def unit_by_bank(quarter, b, first_bank):
+            for u in range(2):
+                acc = bank(first_bank + u)
                 for g in range(LISTS):
-                    for bank, (jt, b) in zip(banks, keys):
-                        first_pass(bank, jt, b, g)
-                        if g == LISTS - 1:
-                            relu_out(bank, jt, b)
-            else:
-                for jt, b in keys:
-                    bank = next_bank()
-                    for g in range(LISTS):
-                        first_pass(bank, jt, b, g)
-                    relu_out(bank, jt, b)
+                    first_passes(acc, quarter, b, u, g)
+                relu_out(acc, quarter, b, u)
+            weave(quarter, b)
+
+        def narrow_unit(first, b, index):
+            quarter, c0 = divmod(first, QUARTER)
+            half, h0 = divmod(first, HALF)
+            acc = bank(index)
+            for t in range(4):
+                for g in range(LISTS):
+                    s0 = 512 * (LISTS * b + g) + P * t
+                    nc.tensor.matmul_mx(
+                        out=acc[:, P * t : P * (t + 1)],
+                        lhsT=w_dealt[g, b][:, 2 * P * t : 2 * P * (t + 1)].bitcast(FP4X4),
+                        lhsT_scale=w_scales[:].bitcast(U8)[:, s0 : s0 + P],
+                        rhs=v_words[g, quarter][:, c0 : c0 + P].bitcast(FP8X4),
+                        rhs_scale=v_scales[g, half][:, h0 : h0 + P],
+                        start=(g == 0),
+                        stop=(g == LISTS - 1),
+                    )
+            nc.scalar.activation(
+                out=grouped[half, b][:, 2 * h0 : 2 * (h0 + P)].bitcast(BF16).rearrange(
+                    "p (c i t) -> p c t i", i=2, t=4
+                ),
+                in_=acc[:].rearrange("p (t c i) -> p c t i", i=2, t=4),
+                func=RELU,
+            )
 
         h_codes, h_scales = {}, {}
 
-        grouped = {}
-
-        def turn(unit, pair, b):
-            if (unit, b) not in grouped:
-                grouped[unit, b] = keep.tile(
-                    [P, P * len(unit), 2], F32, name="grouped%d_%d" % (unit[0], b), align_bytes=64
-                )
-            first = pair[0] - unit[0]
-            turned = next_bank()[:, : 2 * P * len(pair)].rearrange("p (t u j) -> p t u j", u=2, j=P)
-            for place, jt in enumerate(pair):
-                words = h_rows[jt, b][:].bitcast(F32)
-                for u in range(2):
-                    nc.tensor.transpose(turned[:, place, u, :], words[:, P * u : P * (u + 1)], identity[:])
-            nc.scalar.copy(
-                out=grouped[unit, b][:, P * first : P * (first + len(pair)), :].rearrange(
-                    "p (t c i) u -> p t c u i", c=P // 2, i=2
-                ),
-                in_=turned.rearrange("p t u (c i) -> p t c u i", i=2),
-            )
-
-        def quantise(unit, b):
-            width = P * len(unit)
-            codes = keep.tile([P, width], U32, name="h_codes%d_%d" % (unit[0], b), align_bytes=64)
-            scales = keep.tile([P, width], U8, name="h_scales%d_%d" % (unit[0], b), align_bytes=64)
+        def quantise(first, width, b, tag=None):
+            half, c0 = divmod(first, HALF)
+            codes = keep.tile([P, width], U32, name=tag or "h_codes%d_%d" % (first, b), align_bytes=64)
+            scales = keep.tile([P, width], U8, name="h_scales%d_%d" % (first, b), align_bytes=64)
             nc.vector.quantize_mx(
                 out=codes[:].bitcast(FP8X4),
                 scales=scales[:],
-                in_=grouped[unit, b][:].rearrange("p j u -> p (j u)").bitcast(BF16),
+                in_=grouped[half, b][:, 2 * c0 : 2 * (c0 + width)].bitcast(BF16),
             )
-            h_codes[unit, b], h_scales[unit, b] = codes, scales
+            for c in range(0, width, P):
+                h_codes[first + c, b], h_scales[first + c, b] = (codes, c), (scales, c)
 
-        def turn_and_quantise(unit):
-            for b in range(R_PASSES):
-                turn(unit, unit, b)
-                quantise(unit, b)
+        def second_pass(acc, first, width, b, m, start, stop):
+            codes, c0 = h_codes[first, b]
+            scales, c0 = h_scales[first, b]
+            nc.tensor.matmul_mx(
+                out=acc,
+                lhsT=wd[:, b, P * m : P * (m + 1)].bitcast(FP8X4),
+                lhsT_scale=wd_sc[:, b, :].bitcast(U8)[:, P * m : P * (m + 1)],
+                rhs=codes[:, c0 : c0 + width].bitcast(FP8X4),
+                rhs_scale=scales[:, c0 : c0 + width],
+                start=start,
+                stop=stop,
+            )
 
-        def second_layer(unit):
-            width = P * len(unit)
-            cols = slice(P * unit[0], P * unit[0] + width)
-            banks = [next_bank() for m in range(N_TILES)]
-            for b in range(R_PASSES):
-                for m in range(N_TILES):
-                    nc.tensor.matmul_mx(
-                        out=banks[m][:, :width],
-                        lhsT=wd[:, b, P * m : P * (m + 1)].bitcast(FP8X4),
-                        lhsT_scale=wd_sc[:, b, :].bitcast(U8)[:, P * m : P * (m + 1)],
-                        rhs=h_codes[unit, b][:].bitcast(FP8X4),
-                        rhs_scale=h_scales[unit, b][:],
-                        start=(b == 0),
-                        stop=(b == R_PASSES - 1),
-                    )
-            for m in range(N_TILES):
-                nc.vector.tensor_tensor(out=out_sb[:, m, cols], in0=banks[m][:, :width], in1=res_sb[:, m, cols], op=ADD)
+        def store(first, width):
+            cols = slice(first, first + width)
             nc.sync.dma_start(out=out.rearrange("(m p) j -> p m j", p=P)[:, :, cols], in_=out_sb[:, :, cols])
 
-        wide = (0, 1, 2, 3)
-        first_layer((0, 1), by_list=True)
-        first_layer((2,), by_list=False)
-        first_layer((3,), by_list=True)
+        def second_layer_wide(first, first_bank):
+            cols = slice(first, first + HALF)
+            for m in range(N_TILES):
+                acc = bank(first_bank + m)
+                for b in range(R_PASSES):
+                    second_pass(acc[:], first, HALF, b, m, b == 0, b == R_PASSES - 1)
+                nc.vector.tensor_tensor(out=out_sb[:, m, cols], in0=acc[:], in1=res_sb[:, m, cols], op=ADD)
+            store(first, HALF)
+
+        def second_layer(first, width, index):
+            cols = slice(first, first + width)
+            acc = bank(index)[:, : N_TILES * width].rearrange("p (m j) -> p m j", m=N_TILES)
+            for b in range(R_PASSES):
+                for m in range(N_TILES):
+                    second_pass(
+                        acc[:, m, :], first, width, b, m, b == 0 and m == 0, b == R_PASSES - 1 and m == N_TILES - 1
+                    )
+            nc.vector.tensor_tensor(out=out_sb[:, :, cols], in0=acc, in1=res_sb[:, :, cols], op=ADD)
+            store(first, width)
+
+        group_by_list([(0, 0), (1, 0)], 0)
+        group_by_list([(0, 1), (1, 1)], 4)
         gather_scales(1)
-        for b in range(R_PASSES):
-            turn(wide, (0, 1), b)
-        first_layer((4, 5), by_list=True)
-        for b in range(R_PASSES):
-            turn(wide, (2, 3), b)
-            quantise(wide, b)
-        first_layer((6,), by_list=False)
-        turn_and_quantise((4, 5))
-        first_layer((7,), by_list=False)
-        second_layer((0, 1, 2, 3))
-        turn_and_quantise((6,))
-        turn_and_quantise((7,))
-        second_layer((4, 5))
-        second_layer((6,))
-        second_layer((7,))
+        last_words = words_tile("v_words2_1", LISTS * QUARTER)
+        for g in range(LISTS):
+            gather_words(last_words[:, QUARTER * g : QUARTER * (g + 1)], g, 3, QUARTER)
+        group_by_list([(2, 0), (2, 1)], 0)
+        quantise(0, HALF, 0, tag="v_words0_2")
+        quantise(0, HALF, 1, tag="v_words1_2")
+        quantise(2 * QUARTER, QUARTER, 0)
+        quantise(2 * QUARTER, QUARTER, 1)
+        unit_by_bank(3, 0, 4)
+        second_layer_wide(0, 6)
+        quantise(3 * QUARTER, QUARTER, 0)
+        narrow_unit(3 * QUARTER, 1, 0)
+        narrow_unit(3 * QUARTER + P, 1, 1)
+        second_layer(2 * QUARTER, QUARTER, 2)
+        quantise(3 * QUARTER, P, 1)
+        second_layer(3 * QUARTER, P, 3)
+        quantise(3 * QUARTER + P, P, 1)
+        second_layer(3 * QUARTER + P, P, 4)

@@ -196,7 +196,7 @@ def tile_list_rvq_relu_res_kernel(
             half, c0 = divmod(quarter * QUARTER, HALF)
             if c0 == 0:
                 grouped[half, b] = keep.tile([P, 2 * HALF], F32, name="grouped%d_%d" % (half, b), align_bytes=64)
-            copy = nc.gpsimd.tensor_copy if quarter < 3 else nc.scalar.copy
+            copy = nc.vector.tensor_copy if quarter == 2 else nc.scalar.copy
             copy(
                 out=grouped[half, b][:, 2 * c0 : 2 * (c0 + QUARTER)].rearrange("p (c i u) -> p c u i", i=4, u=2),
                 in_=pairs[quarter, b][:].rearrange("p u (c i) -> p c u i", i=4),

@@ -45,43 +45,45 @@ def tile_list_rvq_relu_res_kernel(
         offsets = keep.tile([P, LISTS * J // 16], U16, name="offsets")
         table = keep.tile([P, T], I32, name="table", align_bytes=64)
         table_scales = keep.tile([P, T // 4], I32, name="table_scales", align_bytes=64)
-        staged = keep.tile([P, LISTS * P], I32, name="staged", align_bytes=64)
-        staged_dealt = keep.tile([P, LISTS * P], I32, name="staged_dealt", align_bytes=64)
-        w_scales = keep.tile([P, R_PASSES * LISTS * P], I32, name="w_scales", align_bytes=64)
+        staged_tile = keep.tile([P, LISTS * P], I32, name="staged", align_bytes=64)
+        high_odd = keep.tile([P, LISTS * P + 1], I32, name="w_scales_high", align_bytes=64)
+        low = keep.tile([P, LISTS * P], I32, name="w_scales_low", align_bytes=64)
+        staged = staged_tile[:]
+        w_scales = [low[:], high_odd[:, : LISTS * P]]
         wd = keep.tile([P, R_PASSES, N], I32, name="wd", align_bytes=64)
         wd_sc = keep.tile([P, R_PASSES, N // 4], I32, name="wd_sc", align_bytes=64)
         res_sb = keep.tile([P, N_TILES, J], F32, name="res_sb")
         out_sb = keep.tile([P, N_TILES, J], F32, name="out_sb")
 
-        nc.gpsimd.memset(table_scales[:, : T // 8], 0)
-        nc.vector.memset(table_scales[:, T // 8 :], 0)
-        nc.vector.memset(staged[32:64, :], 0)
-        nc.vector.memset(staged[64:P, :], 0)
-        nc.gpsimd.memset(w_scales[:], 0)
+        warm = keep.tile([P, BANK + BANK // 4 + 64 + 1], I32, name="warm", align_bytes=64)
+        for g in range(LISTS):
+            nc.gpsimd.memset(staged[:, P * g : P * (g + 1)], 0)
+        nc.vector.memset(table_scales[:], 0)
+        nc.vector.memset(warm[:], 0)
+        nc.vector.memset(high_odd[:], 0)
         nc.gpsimd.memset(wd_sc[:], 0)
-        zeros = keep.tile([P, BANK], F32, name="zeros", align_bytes=64)
-        nc.vector.memset(zeros[:], 0.0)
 
+        nc.sync.dma_start(offsets[:], offs)
         for g in range(LISTS):
             nc.sync.dma_start(
-                out=staged[0:32, P * g : P * (g + 1)],
+                out=staged[0:P:4, P * g : P * (g + 1)],
                 in_=w_scales_hbm[g][0].bitcast(I32).rearrange("q (b c) -> (q b) c", b=R_PASSES),
             )
-        nc.gpsimd.tensor_copy(
-            out=staged_dealt[:].bitcast(U8).rearrange("p (g t c i) -> p c g t i", g=LISTS, t=4, i=16),
-            in_=staged[:].bitcast(U8).rearrange("p (g c i t) -> p c g t i", g=LISTS, t=4, i=16),
-        )
+        for g in range(LISTS):
+            cols = slice(512 * g, 512 * (g + 1))
+            engine = nc.gpsimd if g == 0 else nc.vector
+            engine.tensor_copy(
+                out=w_scales[0].bitcast(U8)[:, cols].rearrange("p (t c i) -> p c t i", t=4, i=16),
+                in_=staged.bitcast(U8)[:, cols].rearrange("p (c i t) -> p c t i", t=4, i=16),
+            )
 
         def load_scale_rows(plane, rows):
             for r in range(4):
                 nc.sync.dma_start(out=plane[r:P:32], in_=rows[r:16:4])
 
         def carry_scale_rows(b):
-            for r in range(4):
-                nc.sync.dma_start(
-                    out=w_scales[r:P:32, LISTS * P * b : LISTS * P * (b + 1)],
-                    in_=staged_dealt[2 * r + b : 32 : 8, :],
-                )
+            for r in range(1 - b, 4):
+                nc.sync.dma_start(out=w_scales[b][r:P:32, :], in_=w_scales[0][8 * r + 4 * b : P : 32, :])
 
         w_raw = {}
 
@@ -96,7 +98,6 @@ def tile_list_rvq_relu_res_kernel(
         table_hbm = tab_words[0].rearrange("p t i -> p (t i)").bitcast(I32)
         nc.sync.dma_start(out=table[:, :TABLE_HEAD], in_=table_hbm[:, :TABLE_HEAD])
         load_scale_rows(table_scales, tab_scales[0].bitcast(I32))
-        nc.sync.dma_start(offsets[:], offs)
         nc.sync.dma_start(out=table[:, TABLE_HEAD:], in_=table_hbm[:, TABLE_HEAD:])
         load_weight(0, (0,))
         carry_scale_rows(0)
@@ -114,10 +115,12 @@ def tile_list_rvq_relu_res_kernel(
         for b in range(R_PASSES):
             for g in range(LISTS):
                 dealt = keep.tile([P, 1024], U8, name="w_dealt%d_%d" % (g, b), align_bytes=64)
-                nc.scalar.copy(
-                    out=dealt[:].bitcast(U16).rearrange("p (t c i) -> p c t i", t=4, i=8),
-                    in_=w_raw[g, b].bitcast(U16).rearrange("p (c i t) -> p c t i", t=4, i=8),
-                )
+                parts = (slice(0, 2), slice(2, 4)) if (g, b) == (0, 0) else (slice(0, 4),)
+                for part in parts:
+                    nc.scalar.copy(
+                        out=dealt[:].bitcast(U16).rearrange("p (t c i) -> p c t i", t=4, i=8)[:, :, part, :],
+                        in_=w_raw[g, b].bitcast(U16).rearrange("p (c i t) -> p c t i", t=4, i=8)[:, :, part, :],
+                    )
                 w_dealt[g, b] = dealt
 
         v_words, v_scales = {}, {}
@@ -141,20 +144,18 @@ def tile_list_rvq_relu_res_kernel(
                 v_scales[g, half] = picked
 
         gather_scales(0)
-        zero_codes = keep.tile([P, BANK], U32, name="zero_codes", align_bytes=64)
-        zero_scales = keep.tile([P, BANK], U8, name="zero_scales", align_bytes=64)
-        for part in (slice(0, BANK // 2), slice(BANK // 2, BANK)):
-            nc.vector.quantize_mx(
-                out=zero_codes[:, part].bitcast(FP8X4), scales=zero_scales[:, part], in_=zeros[:].bitcast(BF16)
-            )
+        zero_codes = warm[:, :BANK]
+        zero_scales = warm[:, BANK : BANK + BANK // 4].bitcast(U8)
+        zeros = warm[:, BANK + BANK // 4 : BANK + BANK // 4 + 64].bitcast(BF16)
+        nc.vector.quantize_mx(out=zero_codes[:, :32].bitcast(FP8X4), scales=zero_scales[:, :32], in_=zeros)
         warm_bank = bank(0)
         for warm in range(WARM_PASSES):
             nc.tensor.matmul_mx(
                 out=warm_bank[:],
                 lhsT=zero_codes[:, :P].bitcast(FP8X4),
                 lhsT_scale=v_scales[min(warm, 1), 0][:, :P],
-                rhs=zero_codes[:].bitcast(FP8X4),
-                rhs_scale=zero_scales[:],
+                rhs=zero_codes.bitcast(FP8X4),
+                rhs_scale=zero_scales,
                 start=True,
                 stop=True,
             )
@@ -170,11 +171,11 @@ def tile_list_rvq_relu_res_kernel(
             half, c0 = divmod(quarter * QUARTER, HALF)
             for e in range(2):
                 t = 2 * u + e
-                s0 = 512 * (LISTS * b + g) + P * t
+                s0 = 512 * g + P * t
                 nc.tensor.matmul_mx(
                     out=acc[:, QUARTER * e : QUARTER * (e + 1)],
                     lhsT=w_dealt[g, b][:, 2 * P * t : 2 * P * (t + 1)].bitcast(FP4X4),
-                    lhsT_scale=w_scales[:].bitcast(U8)[:, s0 : s0 + P],
+                    lhsT_scale=w_scales[b].bitcast(U8)[:, s0 : s0 + P],
                     rhs=v_words[g, quarter].bitcast(FP8X4),
                     rhs_scale=v_scales[g, half][:, c0 : c0 + QUARTER],
                     start=(g == 0 and e == 0),
@@ -227,11 +228,11 @@ def tile_list_rvq_relu_res_kernel(
             acc = bank(index)
             for t in range(4):
                 for g in range(LISTS):
-                    s0 = 512 * (LISTS * b + g) + P * t
+                    s0 = 512 * g + P * t
                     nc.tensor.matmul_mx(
                         out=acc[:, P * t : P * (t + 1)],
                         lhsT=w_dealt[g, b][:, 2 * P * t : 2 * P * (t + 1)].bitcast(FP4X4),
-                        lhsT_scale=w_scales[:].bitcast(U8)[:, s0 : s0 + P],
+                        lhsT_scale=w_scales[b].bitcast(U8)[:, s0 : s0 + P],
                         rhs=v_words[g, quarter][:, c0 : c0 + P].bitcast(FP8X4),
                         rhs_scale=v_scales[g, half][:, h0 : h0 + P],
                         start=(g == 0),

@@ -63,8 +63,11 @@ def tile_list_rvq_relu_res_kernel(
         nc.vector.memset(high_odd[:], 0)
         nc.gpsimd.memset(wd_sc[:], 0)
 
+        table_hbm = tab_words[0].rearrange("p t i -> p (t i)").bitcast(I32)
         nc.sync.dma_start(offsets[:], offs)
         for g in range(LISTS):
+            if g == 1:
+                nc.sync.dma_start(out=table[:, :TABLE_HEAD], in_=table_hbm[:, :TABLE_HEAD])
             nc.sync.dma_start(
                 out=staged[0:P:4, P * g : P * (g + 1)],
                 in_=w_scales_hbm[g][0].bitcast(I32).rearrange("q (b c) -> (q b) c", b=R_PASSES),
@@ -95,8 +98,6 @@ def tile_list_rvq_relu_res_kernel(
             for place, b in enumerate(passes):
                 w_raw[g, b] = raw[:, 256 * place : 256 * (place + 1)]
 
-        table_hbm = tab_words[0].rearrange("p t i -> p (t i)").bitcast(I32)
-        nc.sync.dma_start(out=table[:, :TABLE_HEAD], in_=table_hbm[:, :TABLE_HEAD])
         load_scale_rows(table_scales, tab_scales[0].bitcast(I32))
         nc.sync.dma_start(out=table[:, TABLE_HEAD:], in_=table_hbm[:, TABLE_HEAD:])
         load_weight(0, (0,))
@@ -273,29 +274,33 @@ def tile_list_rvq_relu_res_kernel(
                 stop=stop,
             )
 
-        def store(first, width):
+        def store(first, width, rows=slice(0, N_TILES)):
             cols = slice(first, first + width)
-            nc.sync.dma_start(out=out.rearrange("(m p) j -> p m j", p=P)[:, :, cols], in_=out_sb[:, :, cols])
+            nc.sync.dma_start(out=out.rearrange("(m p) j -> p m j", p=P)[:, rows, cols], in_=out_sb[:, rows, cols])
+
+        def second_layer_tile(first, width, m, index):
+            cols = slice(first, first + width)
+            acc = bank(index)[:, :width]
+            for b in range(R_PASSES):
+                second_pass(acc, first, width, b, m, b == 0, b == R_PASSES - 1)
+            nc.vector.tensor_tensor(out=out_sb[:, m, cols], in0=acc, in1=res_sb[:, m, cols], op=ADD)
 
         def second_layer_wide(first, first_bank):
-            cols = slice(first, first + HALF)
             for m in range(N_TILES):
-                acc = bank(first_bank + m)
-                for b in range(R_PASSES):
-                    second_pass(acc[:], first, HALF, b, m, b == 0, b == R_PASSES - 1)
-                nc.vector.tensor_tensor(out=out_sb[:, m, cols], in0=acc[:], in1=res_sb[:, m, cols], op=ADD)
+                second_layer_tile(first, HALF, m, first_bank + m)
             store(first, HALF)
 
-        def second_layer(first, width, index):
-            cols = slice(first, first + width)
-            acc = bank(index)[:, : N_TILES * width].rearrange("p (m j) -> p m j", m=N_TILES)
-            for b in range(R_PASSES):
-                for m in range(N_TILES):
-                    second_pass(
-                        acc[:, m, :], first, width, b, m, b == 0 and m == 0, b == R_PASSES - 1 and m == N_TILES - 1
-                    )
+        def narrow_bank(index):
+            return bank(index)[:, : N_TILES * P].rearrange("p (m j) -> p m j", m=N_TILES)
+
+        def narrow_passes(acc, first, b):
+            for m in range(N_TILES):
+                second_pass(acc[:, m, :], first, P, b, m, b == 0 and m == 0, b == R_PASSES - 1 and m == N_TILES - 1)
+
+        def narrow_out(acc, first):
+            cols = slice(first, first + P)
             nc.vector.tensor_tensor(out=out_sb[:, :, cols], in0=acc, in1=res_sb[:, :, cols], op=ADD)
-            store(first, width)
+            store(first, P)
 
         group_by_list([(0, 0), (1, 0)], 0)
         group_by_list([(0, 1), (1, 1)], 4)
@@ -312,9 +317,17 @@ def tile_list_rvq_relu_res_kernel(
         second_layer_wide(0, 6)
         quantise(3 * QUARTER, QUARTER, 0)
         narrow_unit(3 * QUARTER, 1, 0)
-        narrow_unit(3 * QUARTER + P, 1, 1)
-        second_layer(2 * QUARTER, QUARTER, 2)
+        second_layer_tile(2 * QUARTER, QUARTER, 0, 2)
+        store(2 * QUARTER, QUARTER, slice(0, 1))
         quantise(3 * QUARTER, P, 1)
-        second_layer(3 * QUARTER, P, 3)
+        narrow_unit(3 * QUARTER + P, 1, 1)
+        before_last, last = narrow_bank(4), narrow_bank(5)
+        for b in range(R_PASSES):
+            narrow_passes(before_last, 3 * QUARTER, b)
+        narrow_out(before_last, 3 * QUARTER)
+        narrow_passes(last, 3 * QUARTER + P, 0)
         quantise(3 * QUARTER + P, P, 1)
-        second_layer(3 * QUARTER + P, P, 4)
+        second_layer_tile(2 * QUARTER, QUARTER, 1, 3)
+        store(2 * QUARTER, QUARTER, slice(1, 2))
+        narrow_passes(last, 3 * QUARTER + P, 1)
+        narrow_out(last, 3 * QUARTER + P)

@@ -102,9 +102,10 @@ def tile_list_rvq_relu_res_kernel(
         nc.sync.dma_start(out=table[:, TABLE_HEAD:], in_=table_hbm[:, TABLE_HEAD:])
         load_weight(0, (0,))
         carry_scale_rows(0)
-        load_weight(1, (0, 1))
+        load_weight(1, (0,))
         load_weight(2, (0, 1))
         load_weight(0, (1,))
+        load_weight(1, (1,))
         carry_scale_rows(1)
         load_scale_rows(wd_sc, wd_scales.bitcast(I32).rearrange("a q n -> q a n"))
         nc.sync.dma_start(
@@ -150,11 +151,11 @@ def tile_list_rvq_relu_res_kernel(
         zeros = warm[:, BANK + BANK // 4 : BANK + BANK // 4 + 64].bitcast(BF16)
         nc.vector.quantize_mx(out=zero_codes[:, :32].bitcast(FP8X4), scales=zero_scales[:, :32], in_=zeros)
         warm_bank = bank(0)
-        for warm in range(WARM_PASSES):
+        for warm_pass in range(WARM_PASSES):
             nc.tensor.matmul_mx(
                 out=warm_bank[:],
                 lhsT=zero_codes[:, :P].bitcast(FP8X4),
-                lhsT_scale=v_scales[min(warm, 1), 0][:, :P],
+                lhsT_scale=v_scales[warm_pass // 2, 0][:, :P],
                 rhs=zero_codes.bitcast(FP8X4),
                 rhs_scale=zero_scales,
                 start=True,
@@ -300,7 +301,6 @@ def tile_list_rvq_relu_res_kernel(
         def narrow_out(acc, first):
             cols = slice(first, first + P)
             nc.vector.tensor_tensor(out=out_sb[:, :, cols], in0=acc, in1=res_sb[:, :, cols], op=ADD)
-            store(first, P)
 
         group_by_list([(0, 0), (1, 0)], 0)
         group_by_list([(0, 1), (1, 1)], 4)
@@ -318,16 +318,17 @@ def tile_list_rvq_relu_res_kernel(
         quantise(3 * QUARTER, QUARTER, 0)
         narrow_unit(3 * QUARTER, 1, 0)
         second_layer_tile(2 * QUARTER, QUARTER, 0, 2)
-        store(2 * QUARTER, QUARTER, slice(0, 1))
         quantise(3 * QUARTER, P, 1)
         narrow_unit(3 * QUARTER + P, 1, 1)
         before_last, last = narrow_bank(4), narrow_bank(5)
         for b in range(R_PASSES):
             narrow_passes(before_last, 3 * QUARTER, b)
         narrow_out(before_last, 3 * QUARTER)
+        store(2 * QUARTER, QUARTER + P, slice(0, 1))
         narrow_passes(last, 3 * QUARTER + P, 0)
         quantise(3 * QUARTER + P, P, 1)
         second_layer_tile(2 * QUARTER, QUARTER, 1, 3)
-        store(2 * QUARTER, QUARTER, slice(1, 2))
+        store(2 * QUARTER, QUARTER + P, slice(1, 2))
         narrow_passes(last, 3 * QUARTER + P, 1)
         narrow_out(last, 3 * QUARTER + P)
+        store(3 * QUARTER + P, P)

@@ -74,7 +74,7 @@ def tile_list_rvq_relu_res_kernel(
             )
         for g in range(LISTS):
             cols = slice(512 * g, 512 * (g + 1))
-            engine = nc.gpsimd if g == 0 else nc.vector
+            engine = nc.gpsimd if g < LISTS - 1 else nc.vector
             engine.tensor_copy(
                 out=w_scales[0].bitcast(U8)[:, cols].rearrange("p (t c i) -> p c t i", t=4, i=16),
                 in_=staged.bitcast(U8)[:, cols].rearrange("p (c i t) -> p c t i", t=4, i=16),

@@ -46,12 +46,12 @@ def tile_list_rvq_relu_res_kernel(
         table = keep.tile([P, T], I32, name="table", align_bytes=64)
         table_scales = keep.tile([P, T // 4], I32, name="table_scales", align_bytes=64)
         staged_tile = keep.tile([P, LISTS * P], I32, name="staged", align_bytes=64)
-        high_odd = keep.tile([P, LISTS * P + 1], I32, name="w_scales_high", align_bytes=64)
-        low = keep.tile([P, LISTS * P], I32, name="w_scales_low", align_bytes=64)
+        high_odd = keep.tile([P, LISTS * P + 1], I32, name="w_scales_high", align_bytes=256)
+        low = keep.tile([P, LISTS * P], I32, name="w_scales_low", align_bytes=256)
         staged = staged_tile[:]
         w_scales = [low[:], high_odd[:, : LISTS * P]]
-        wd = keep.tile([P, R_PASSES, N], I32, name="wd", align_bytes=64)
-        wd_sc = keep.tile([P, R_PASSES, N // 4], I32, name="wd_sc", align_bytes=64)
+        wd = keep.tile([P, R_PASSES, N], I32, name="wd", align_bytes=256)
+        wd_sc = keep.tile([P, R_PASSES, N // 4], I32, name="wd_sc", align_bytes=256)
         res_sb = keep.tile([P, N_TILES, J], F32, name="res_sb")
         out_sb = keep.tile([P, N_TILES, J], F32, name="out_sb")
 
@@ -116,7 +116,7 @@ def tile_list_rvq_relu_res_kernel(
         w_dealt = {}
         for b in range(R_PASSES):
             for g in range(LISTS):
-                dealt = keep.tile([P, 1024], U8, name="w_dealt%d_%d" % (g, b), align_bytes=64)
+                dealt = keep.tile([P, 1024], U8, name="w_dealt%d_%d" % (g, b), align_bytes=256)
                 parts = (slice(0, 2), slice(2, 4)) if (g, b) == (0, 0) else (slice(0, 4),)
                 for part in parts:
                     nc.scalar.copy(
@@ -137,11 +137,11 @@ def tile_list_rvq_relu_res_kernel(
                 v_words[g, first_quarter + c0 // QUARTER] = picked[:, c0 : c0 + QUARTER]
 
         def words_tile(name, width):
-            return keep.tile([P, width], U32, name=name, align_bytes=64)
+            return keep.tile([P, width], U32, name=name, align_bytes=256)
 
         def gather_scales(half):
             for g in range(LISTS):
-                picked = keep.tile([P, HALF], U8, name="v_scales%d" % g, align_bytes=64)
+                picked = keep.tile([P, HALF], U8, name="v_scales%d" % g, align_bytes=256)
                 gather(picked[:], table_scales[:].bitcast(U8), g, half * HALF, HALF)
                 v_scales[g, half] = picked
 
@@ -252,8 +252,8 @@ def tile_list_rvq_relu_res_kernel(
 
         def quantise(first, width, b, tag=None):
             half, c0 = divmod(first, HALF)
-            codes = keep.tile([P, width], U32, name=tag or "h_codes%d_%d" % (first, b), align_bytes=64)
-            scales = keep.tile([P, width], U8, name="h_scales%d_%d" % (first, b), align_bytes=64)
+            codes = keep.tile([P, width], U32, name=tag or "h_codes%d_%d" % (first, b), align_bytes=256)
+            scales = keep.tile([P, width], U8, name="h_scales%d_%d" % (first, b), align_bytes=256)
             nc.vector.quantize_mx(
                 out=codes[:].bitcast(FP8X4),
                 scales=scales[:],

@@ -1,4 +1,5 @@
 from contextlib import ExitStack
+from itertools import product
 
 import concourse.mybir as mybir
 
@@ -25,6 +26,7 @@ R_PASSES = R // 512
 N_TILES = N // P
 WARM_PASSES = 5
 TABLE_HEAD = 640
+TABLE_TAIL = 2048
 
 
 def tile_list_rvq_relu_res_kernel(
@@ -46,21 +48,21 @@ def tile_list_rvq_relu_res_kernel(
         table = keep.tile([P, T], I32, name="table", align_bytes=64)
         table_scales = keep.tile([P, T // 4], I32, name="table_scales", align_bytes=64)
         staged_tile = keep.tile([P, LISTS * P], I32, name="staged", align_bytes=64)
-        high_odd = keep.tile([P, LISTS * P + 1], I32, name="w_scales_high", align_bytes=256)
+        high = keep.tile([P, LISTS * P], I32, name="w_scales_high", align_bytes=256)
         low = keep.tile([P, LISTS * P], I32, name="w_scales_low", align_bytes=256)
         staged = staged_tile[:]
-        w_scales = [low[:], high_odd[:, : LISTS * P]]
-        wd = keep.tile([P, R_PASSES, N], I32, name="wd", align_bytes=256)
+        w_scales = [low[:], high[:]]
         wd_sc = keep.tile([P, R_PASSES, N // 4], I32, name="wd_sc", align_bytes=256)
+        wd = keep.tile([P, R_PASSES, N], I32, name="wd", align_bytes=256)
         res_sb = keep.tile([P, N_TILES, J], F32, name="res_sb")
         out_sb = keep.tile([P, N_TILES, J], F32, name="out_sb")
 
-        warm = keep.tile([P, BANK + BANK // 4 + 64 + 1], I32, name="warm", align_bytes=64)
+        warm = keep.tile([P, 2 * P + 64], I32, name="warm", align_bytes=64)
         for g in range(LISTS):
             nc.gpsimd.memset(staged[:, P * g : P * (g + 1)], 0)
         nc.vector.memset(table_scales[:], 0)
         nc.vector.memset(warm[:], 0)
-        nc.vector.memset(high_odd[:], 0)
+        nc.vector.memset(high[:], 0)
         nc.gpsimd.memset(wd_sc[:], 0)
 
         table_hbm = tab_words[0].rearrange("p t i -> p (t i)").bitcast(I32)
@@ -84,14 +86,18 @@ def tile_list_rvq_relu_res_kernel(
             for r in range(4):
                 nc.sync.dma_start(out=plane[r:P:32], in_=rows[r:16:4])
 
-        def carry_scale_rows(b):
-            for r in range(1 - b, 4):
-                nc.sync.dma_start(out=w_scales[b][r:P:32, :], in_=w_scales[0][8 * r + 4 * b : P : 32, :])
+        def carry_low_rows():
+            for r in range(1, 4):
+                nc.sync.dma_start(out=w_scales[0][r:P:32, :], in_=w_scales[0][8 * r : P : 32, :])
+
+        def carry_high_rows():
+            for r in range(4):
+                nc.sync.dma_start(out=high[r:P:32, :], in_=low[8 * r + 4 : P : 32, :])
 
         w_raw = {}
 
         def load_weight(g, passes):
-            raw = keep.tile([P, 256 * len(passes)], I32, name="w_raw%d_%d" % (g, passes[0]), align_bytes=64)
+            raw = keep.tile([P, 256 * len(passes)], I32, name="w_raw%d_%d" % (g, passes[0]), align_bytes=256)
             nc.sync.dma_start(
                 out=raw[:], in_=w_words_hbm[g][0].bitcast(I32)[:, 256 * passes[0] : 256 * (passes[-1] + 1)]
             )
@@ -99,31 +105,44 @@ def tile_list_rvq_relu_res_kernel(
                 w_raw[g, b] = raw[:, 256 * place : 256 * (place + 1)]
 
         load_scale_rows(table_scales, tab_scales[0].bitcast(I32))
-        nc.sync.dma_start(out=table[:, TABLE_HEAD:], in_=table_hbm[:, TABLE_HEAD:])
+        nc.sync.dma_start(out=table[:, TABLE_HEAD:TABLE_TAIL], in_=table_hbm[:, TABLE_HEAD:TABLE_TAIL])
         load_weight(0, (0,))
-        carry_scale_rows(0)
-        load_weight(1, (0,))
+        nc.sync.dma_start(out=table[:, TABLE_TAIL:], in_=table_hbm[:, TABLE_TAIL:])
+        carry_low_rows()
+        load_weight(1, (0, 1))
         load_weight(2, (0, 1))
         load_weight(0, (1,))
-        load_weight(1, (1,))
-        carry_scale_rows(1)
+        carry_high_rows()
         load_scale_rows(wd_sc, wd_scales.bitcast(I32).rearrange("a q n -> q a n"))
         nc.sync.dma_start(
             out=wd[:], in_=wd_words.rearrange("a p n i -> p a (n i)").bitcast(I32)
         )
         nc.sync.dma_start(out=res_sb[:], in_=res.rearrange("(m p) j -> p m j", p=P))
 
+        zeros = warm[:, :64].bitcast(BF16)
+        zero_codes = warm[:, 64 : 64 + P]
+        zero_scales = warm[:, 64 + P :].bitcast(U8)
+        nc.vector.quantize_mx(out=zero_codes[:, :32].bitcast(FP8X4), scales=zero_scales[:, :32], in_=zeros)
+        warm_bank = bank(0)
+        for warm_pass in range(WARM_PASSES):
+            nc.tensor.matmul_mx(
+                out=warm_bank[:],
+                lhsT=zero_codes.bitcast(FP8X4),
+                lhsT_scale=zero_scales[:, :P],
+                rhs=w_raw[0, 0].bitcast(U8).bitcast(FP4X4),
+                rhs_scale=zero_scales,
+                start=True,
+                stop=True,
+            )
+
         w_dealt = {}
-        for b in range(R_PASSES):
-            for g in range(LISTS):
-                dealt = keep.tile([P, 1024], U8, name="w_dealt%d_%d" % (g, b), align_bytes=256)
-                parts = (slice(0, 2), slice(2, 4)) if (g, b) == (0, 0) else (slice(0, 4),)
-                for part in parts:
-                    nc.scalar.copy(
-                        out=dealt[:].bitcast(U16).rearrange("p (t c i) -> p c t i", t=4, i=8)[:, :, part, :],
-                        in_=w_raw[g, b].bitcast(U16).rearrange("p (c i t) -> p c t i", t=4, i=8)[:, :, part, :],
-                    )
-                w_dealt[g, b] = dealt
+        for b, g in product(range(R_PASSES), range(LISTS)):
+            dealt = keep.tile([P, 1024], U8, name="w_dealt%d_%d" % (g, b), align_bytes=256)
+            nc.scalar.copy(
+                out=dealt[:].bitcast(U16).rearrange("p (t c i) -> p c t i", t=4, i=8),
+                in_=w_raw[g, b].bitcast(U16).rearrange("p (c i t) -> p c t i", t=4, i=8),
+            )
+            w_dealt[g, b] = dealt
 
         v_words, v_scales = {}, {}
 
@@ -139,28 +158,13 @@ def tile_list_rvq_relu_res_kernel(
         def words_tile(name, width):
             return keep.tile([P, width], U32, name=name, align_bytes=256)
 
-        def gather_scales(half):
-            for g in range(LISTS):
-                picked = keep.tile([P, HALF], U8, name="v_scales%d" % g, align_bytes=256)
-                gather(picked[:], table_scales[:].bitcast(U8), g, half * HALF, HALF)
-                v_scales[g, half] = picked
+        def gather_scales(g, half):
+            picked = keep.tile([P, HALF], U8, name="v_scales%d" % g, align_bytes=256)
+            gather(picked[:], table_scales[:].bitcast(U8), g, half * HALF, HALF)
+            v_scales[g, half] = picked
 
-        gather_scales(0)
-        zero_codes = warm[:, :BANK]
-        zero_scales = warm[:, BANK : BANK + BANK // 4].bitcast(U8)
-        zeros = warm[:, BANK + BANK // 4 : BANK + BANK // 4 + 64].bitcast(BF16)
-        nc.vector.quantize_mx(out=zero_codes[:, :32].bitcast(FP8X4), scales=zero_scales[:, :32], in_=zeros)
-        warm_bank = bank(0)
-        for warm_pass in range(WARM_PASSES):
-            nc.tensor.matmul_mx(
-                out=warm_bank[:],
-                lhsT=zero_codes[:, :P].bitcast(FP8X4),
-                lhsT_scale=v_scales[warm_pass // 2, 0][:, :P],
-                rhs=zero_codes.bitcast(FP8X4),
-                rhs_scale=zero_scales,
-                start=True,
-                stop=True,
-            )
+        for g in range(LISTS):
+            gather_scales(g, 0)
         for g in range(LISTS):
             for quarter in range(2):
                 gather_words(words_tile("v_words%d_%d" % (g, quarter), QUARTER)[:], g, quarter, QUARTER)
@@ -304,7 +308,8 @@ def tile_list_rvq_relu_res_kernel(
 
         group_by_list([(0, 0), (1, 0)], 0)
         group_by_list([(0, 1), (1, 1)], 4)
-        gather_scales(1)
+        for g in range(LISTS):
+            gather_scales(g, 1)
         last_words = words_tile("v_words2_1", LISTS * QUARTER)
         for g in range(LISTS):
             gather_words(last_words[:, QUARTER * g : QUARTER * (g + 1)], g, 3, QUARTER)

@@ -25,7 +25,7 @@ BANK = 512
 R_PASSES = R // 512
 N_TILES = N // P
 WARM_PASSES = 5
-TABLE_HEAD = 640
+TABLE_HEAD = 1024
 TABLE_TAIL = 2048
 
 

@@ -25,8 +25,8 @@ BANK = 512
 R_PASSES = R // 512
 N_TILES = N // P
 WARM_PASSES = 5
-TABLE_HEAD = 1024
-TABLE_TAIL = 2048
+TABLE_HEAD = 640
+TABLE_TAIL = 2304
 
 
 def tile_list_rvq_relu_res_kernel(
@@ -57,7 +57,7 @@ def tile_list_rvq_relu_res_kernel(
         res_sb = keep.tile([P, N_TILES, J], F32, name="res_sb")
         out_sb = keep.tile([P, N_TILES, J], F32, name="out_sb")
 
-        warm = keep.tile([P, 2 * P + 64], I32, name="warm", align_bytes=64)
+        warm = keep.tile([P, 64 + BANK + BANK // 4], I32, name="warm", align_bytes=64)
         for g in range(LISTS):
             nc.gpsimd.memset(staged[:, P * g : P * (g + 1)], 0)
         nc.vector.memset(table_scales[:], 0)
@@ -82,8 +82,8 @@ def tile_list_rvq_relu_res_kernel(
                 in_=staged.bitcast(U8)[:, cols].rearrange("p (c i t) -> p c t i", t=4, i=16),
             )
 
-        def load_scale_rows(plane, rows):
-            for r in range(4):
+        def load_scale_rows(plane, rows, which=range(4)):
+            for r in which:
                 nc.sync.dma_start(out=plane[r:P:32], in_=rows[r:16:4])
 
         def carry_low_rows():
@@ -93,6 +93,23 @@ def tile_list_rvq_relu_res_kernel(
         def carry_high_rows():
             for r in range(4):
                 nc.sync.dma_start(out=high[r:P:32, :], in_=low[8 * r + 4 : P : 32, :])
+
+        def warm_up():
+            zeros = warm[:, :64].bitcast(BF16)
+            zero_codes = warm[:, 64 : 64 + BANK]
+            zero_scales = warm[:, 64 + BANK :].bitcast(U8)
+            nc.vector.quantize_mx(out=zero_codes[:, :32].bitcast(FP8X4), scales=zero_scales[:, :32], in_=zeros)
+            warm_bank = bank(0)
+            for warm_pass in range(WARM_PASSES):
+                nc.tensor.matmul_mx(
+                    out=warm_bank[:],
+                    lhsT=zero_codes[:, :P].bitcast(FP8X4),
+                    lhsT_scale=wd_sc[:, 0, :].bitcast(U8)[:, :P],
+                    rhs=zero_codes.bitcast(FP8X4),
+                    rhs_scale=zero_scales,
+                    start=True,
+                    stop=True,
+                )
 
         w_raw = {}
 
@@ -106,42 +123,31 @@ def tile_list_rvq_relu_res_kernel(
 
         load_scale_rows(table_scales, tab_scales[0].bitcast(I32))
         nc.sync.dma_start(out=table[:, TABLE_HEAD:TABLE_TAIL], in_=table_hbm[:, TABLE_HEAD:TABLE_TAIL])
-        load_weight(0, (0,))
+        wd_scale_rows = wd_scales.bitcast(I32).rearrange("a q n -> q a n")
+        load_scale_rows(wd_sc, wd_scale_rows, range(1))
         nc.sync.dma_start(out=table[:, TABLE_TAIL:], in_=table_hbm[:, TABLE_TAIL:])
+        warm_up()
+        load_weight(0, (0,))
         carry_low_rows()
         load_weight(1, (0, 1))
         load_weight(2, (0, 1))
         load_weight(0, (1,))
         carry_high_rows()
-        load_scale_rows(wd_sc, wd_scales.bitcast(I32).rearrange("a q n -> q a n"))
+        load_scale_rows(wd_sc, wd_scale_rows, range(1, 4))
         nc.sync.dma_start(
             out=wd[:], in_=wd_words.rearrange("a p n i -> p a (n i)").bitcast(I32)
         )
         nc.sync.dma_start(out=res_sb[:], in_=res.rearrange("(m p) j -> p m j", p=P))
 
-        zeros = warm[:, :64].bitcast(BF16)
-        zero_codes = warm[:, 64 : 64 + P]
-        zero_scales = warm[:, 64 + P :].bitcast(U8)
-        nc.vector.quantize_mx(out=zero_codes[:, :32].bitcast(FP8X4), scales=zero_scales[:, :32], in_=zeros)
-        warm_bank = bank(0)
-        for warm_pass in range(WARM_PASSES):
-            nc.tensor.matmul_mx(
-                out=warm_bank[:],
-                lhsT=zero_codes.bitcast(FP8X4),
-                lhsT_scale=zero_scales[:, :P],
-                rhs=w_raw[0, 0].bitcast(U8).bitcast(FP4X4),
-                rhs_scale=zero_scales,
-                start=True,
-                stop=True,
-            )
-
         w_dealt = {}
         for b, g in product(range(R_PASSES), range(LISTS)):
             dealt = keep.tile([P, 1024], U8, name="w_dealt%d_%d" % (g, b), align_bytes=256)
-            nc.scalar.copy(
-                out=dealt[:].bitcast(U16).rearrange("p (t c i) -> p c t i", t=4, i=8),
-                in_=w_raw[g, b].bitcast(U16).rearrange("p (c i t) -> p c t i", t=4, i=8),
-            )
+            parts = (slice(0, 2), slice(2, 4)) if (g, b) == (0, 0) else (slice(0, 4),)
+            for part in parts:
+                nc.scalar.copy(
+                    out=dealt[:].bitcast(U16).rearrange("p (t c i) -> p c t i", t=4, i=8)[:, :, part, :],
+                    in_=w_raw[g, b].bitcast(U16).rearrange("p (c i t) -> p c t i", t=4, i=8)[:, :, part, :],
+                )
             w_dealt[g, b] = dealt
 
         v_words, v_scales = {}, {}
@@ -322,16 +328,16 @@ def tile_list_rvq_relu_res_kernel(
         second_layer_wide(0, 6)
         quantise(3 * QUARTER, QUARTER, 0)
         narrow_unit(3 * QUARTER, 1, 0)
-        second_layer_tile(2 * QUARTER, QUARTER, 0, 2)
         quantise(3 * QUARTER, P, 1)
         narrow_unit(3 * QUARTER + P, 1, 1)
+        second_layer_tile(2 * QUARTER, QUARTER, 0, 2)
         before_last, last = narrow_bank(4), narrow_bank(5)
         for b in range(R_PASSES):
             narrow_passes(before_last, 3 * QUARTER, b)
-        narrow_out(before_last, 3 * QUARTER)
-        store(2 * QUARTER, QUARTER + P, slice(0, 1))
         narrow_passes(last, 3 * QUARTER + P, 0)
         quantise(3 * QUARTER + P, P, 1)
+        narrow_out(before_last, 3 * QUARTER)
+        store(2 * QUARTER, QUARTER + P, slice(0, 1))
         second_layer_tile(2 * QUARTER, QUARTER, 1, 3)
         store(2 * QUARTER, QUARTER + P, slice(1, 2))
         narrow_passes(last, 3 * QUARTER + P, 1)

@@ -48,11 +48,11 @@ def tile_list_rvq_relu_res_kernel(
         table = keep.tile([P, T], I32, name="table", align_bytes=64)
         table_scales = keep.tile([P, T // 4], I32, name="table_scales", align_bytes=64)
         staged_tile = keep.tile([P, LISTS * P], I32, name="staged", align_bytes=64)
-        high = keep.tile([P, LISTS * P], I32, name="w_scales_high", align_bytes=256)
-        low = keep.tile([P, LISTS * P], I32, name="w_scales_low", align_bytes=256)
+        high = keep.tile([P, (LISTS + 1) * P], I32, name="w_scales_high", align_bytes=256)
+        low = keep.tile([P, (LISTS + 1) * P], I32, name="w_scales_low", align_bytes=256)
         staged = staged_tile[:]
-        w_scales = [low[:], high[:]]
-        wd_sc = keep.tile([P, R_PASSES, N // 4], I32, name="wd_sc", align_bytes=256)
+        w_scales = [low[:, : LISTS * P], high[:, : LISTS * P]]
+        wd_staged, wd_sc = low[:, LISTS * P :], high[:, LISTS * P :].bitcast(U8)
         wd = keep.tile([P, R_PASSES, N], I32, name="wd", align_bytes=256)
         res_sb = keep.tile([P, N_TILES, J], F32, name="res_sb")
         out_sb = keep.tile([P, N_TILES, J], F32, name="out_sb")
@@ -63,7 +63,7 @@ def tile_list_rvq_relu_res_kernel(
         nc.vector.memset(table_scales[:], 0)
         nc.vector.memset(warm[:], 0)
         nc.vector.memset(high[:], 0)
-        nc.gpsimd.memset(wd_sc[:], 0)
+        nc.gpsimd.memset(wd_staged, 0)
 
         table_hbm = tab_words[0].rearrange("p t i -> p (t i)").bitcast(I32)
         nc.sync.dma_start(offsets[:], offs)
@@ -82,8 +82,8 @@ def tile_list_rvq_relu_res_kernel(
                 in_=staged.bitcast(U8)[:, cols].rearrange("p (c i t) -> p c t i", t=4, i=16),
             )
 
-        def load_scale_rows(plane, rows, which=range(4)):
-            for r in which:
+        def load_scale_rows(plane, rows):
+            for r in range(4):
                 nc.sync.dma_start(out=plane[r:P:32], in_=rows[r:16:4])
 
         def carry_low_rows():
@@ -104,7 +104,7 @@ def tile_list_rvq_relu_res_kernel(
                 nc.tensor.matmul_mx(
                     out=warm_bank[:],
                     lhsT=zero_codes[:, :P].bitcast(FP8X4),
-                    lhsT_scale=wd_sc[:, 0, :].bitcast(U8)[:, :P],
+                    lhsT_scale=(zero_scales if warm_pass else wd_staged.bitcast(U8))[:, :P],
                     rhs=zero_codes.bitcast(FP8X4),
                     rhs_scale=zero_scales,
                     start=True,
@@ -123,17 +123,19 @@ def tile_list_rvq_relu_res_kernel(
 
         load_scale_rows(table_scales, tab_scales[0].bitcast(I32))
         nc.sync.dma_start(out=table[:, TABLE_HEAD:TABLE_TAIL], in_=table_hbm[:, TABLE_HEAD:TABLE_TAIL])
-        wd_scale_rows = wd_scales.bitcast(I32).rearrange("a q n -> q a n")
-        load_scale_rows(wd_sc, wd_scale_rows, range(1))
+        nc.sync.dma_start(
+            out=wd_staged[4:P:8].rearrange("q (a n) -> q a n", a=R_PASSES),
+            in_=wd_scales.bitcast(I32).rearrange("a q n -> q a n"),
+        )
         nc.sync.dma_start(out=table[:, TABLE_TAIL:], in_=table_hbm[:, TABLE_TAIL:])
         warm_up()
         load_weight(0, (0,))
         carry_low_rows()
-        load_weight(1, (0, 1))
+        load_weight(1, (0,))
         load_weight(2, (0, 1))
         load_weight(0, (1,))
+        load_weight(1, (1,))
         carry_high_rows()
-        load_scale_rows(wd_sc, wd_scale_rows, range(1, 4))
         nc.sync.dma_start(
             out=wd[:], in_=wd_words.rearrange("a p n i -> p a (n i)").bitcast(I32)
         )
@@ -258,6 +260,31 @@ def tile_list_rvq_relu_res_kernel(
                 func=RELU,
             )
 
+        def last_unit(first, b, banks):
+            quarter, c0 = divmod(first, QUARTER)
+            half, h0 = divmod(first, HALF)
+            woven = grouped[half, b][:, 2 * h0 : 2 * (h0 + P)].bitcast(BF16).rearrange("p (c i t) -> p c t i", i=2, t=4)
+            for u, index in enumerate(banks):
+                acc = bank(index)[:, : 2 * P]
+                for e in range(2):
+                    t = 2 * u + e
+                    for g in range(LISTS):
+                        s0 = 512 * g + P * t
+                        nc.tensor.matmul_mx(
+                            out=acc[:, P * e : P * (e + 1)],
+                            lhsT=w_dealt[g, b][:, 2 * P * t : 2 * P * (t + 1)].bitcast(FP4X4),
+                            lhsT_scale=w_scales[b].bitcast(U8)[:, s0 : s0 + P],
+                            rhs=v_words[g, quarter][:, c0 : c0 + P].bitcast(FP8X4),
+                            rhs_scale=v_scales[g, half][:, h0 : h0 + P],
+                            start=(g == 0),
+                            stop=(g == LISTS - 1),
+                        )
+                nc.scalar.activation(
+                    out=woven[:, :, 2 * u : 2 * u + 2, :],
+                    in_=acc.rearrange("p (t c i) -> p c t i", i=2, t=2),
+                    func=RELU,
+                )
+
         h_codes, h_scales = {}, {}
 
         def quantise(first, width, b, tag=None):
@@ -278,7 +305,7 @@ def tile_list_rvq_relu_res_kernel(
             nc.tensor.matmul_mx(
                 out=acc,
                 lhsT=wd[:, b, P * m : P * (m + 1)].bitcast(FP8X4),
-                lhsT_scale=wd_sc[:, b, :].bitcast(U8)[:, P * m : P * (m + 1)],
+                lhsT_scale=wd_sc[:, N * b + P * m : N * b + P * (m + 1)],
                 rhs=codes[:, c0 : c0 + width].bitcast(FP8X4),
                 rhs_scale=scales[:, c0 : c0 + width],
                 start=start,
@@ -295,11 +322,11 @@ def tile_list_rvq_relu_res_kernel(
             for b in range(R_PASSES):
                 second_pass(acc, first, width, b, m, b == 0, b == R_PASSES - 1)
             nc.vector.tensor_tensor(out=out_sb[:, m, cols], in0=acc, in1=res_sb[:, m, cols], op=ADD)
+            store(first, width, slice(m, m + 1))
 
         def second_layer_wide(first, first_bank):
             for m in range(N_TILES):
                 second_layer_tile(first, HALF, m, first_bank + m)
-            store(first, HALF)
 
         def narrow_bank(index):
             return bank(index)[:, : N_TILES * P].rearrange("p (m j) -> p m j", m=N_TILES)
@@ -329,17 +356,16 @@ def tile_list_rvq_relu_res_kernel(
         quantise(3 * QUARTER, QUARTER, 0)
         narrow_unit(3 * QUARTER, 1, 0)
         quantise(3 * QUARTER, P, 1)
-        narrow_unit(3 * QUARTER + P, 1, 1)
+        last_unit(3 * QUARTER + P, 1, (1, 6))
         second_layer_tile(2 * QUARTER, QUARTER, 0, 2)
+        quantise(3 * QUARTER + P, P, 1)
+        second_layer_tile(2 * QUARTER, QUARTER, 1, 3)
         before_last, last = narrow_bank(4), narrow_bank(5)
         for b in range(R_PASSES):
             narrow_passes(before_last, 3 * QUARTER, b)
-        narrow_passes(last, 3 * QUARTER + P, 0)
-        quantise(3 * QUARTER + P, P, 1)
         narrow_out(before_last, 3 * QUARTER)
-        store(2 * QUARTER, QUARTER + P, slice(0, 1))
-        second_layer_tile(2 * QUARTER, QUARTER, 1, 3)
-        store(2 * QUARTER, QUARTER + P, slice(1, 2))
-        narrow_passes(last, 3 * QUARTER + P, 1)
+        store(3 * QUARTER, P)
+        for b in range(R_PASSES):
+            narrow_passes(last, 3 * QUARTER + P, b)
         narrow_out(last, 3 * QUARTER + P)
         store(3 * QUARTER + P, P)

@@ -25,7 +25,7 @@ BANK = 512
 R_PASSES = R // 512
 N_TILES = N // P
 WARM_PASSES = 5
-TABLE_HEAD = 640
+TABLE_HEAD = 448
 TABLE_TAIL = 2304
 
 

@@ -166,18 +166,18 @@ def tile_list_rvq_relu_res_kernel(
         def words_tile(name, width):
             return keep.tile([P, width], U32, name=name, align_bytes=256)
 
-        def gather_scales(g, half):
-            picked = keep.tile([P, HALF], U8, name="v_scales%d" % g, align_bytes=256)
+        def gather_scales(g, half, place):
+            picked = keep.tile([P, HALF], U8, name=place, align_bytes=256)
             gather(picked[:], table_scales[:].bitcast(U8), g, half * HALF, HALF)
             v_scales[g, half] = picked
 
+        half_words = {}
         for g in range(LISTS):
-            gather_scales(g, 0)
+            gather_scales(g, 0, "v_scales%d" % g)
         for g in range(LISTS):
+            half_words[g, 0] = words_tile("v_words%d" % g, HALF)
             for quarter in range(2):
-                gather_words(words_tile("v_words%d_%d" % (g, quarter), QUARTER)[:], g, quarter, QUARTER)
-        for g in range(LISTS):
-            gather_words(words_tile("v_words%d_2" % g, QUARTER)[:], g, 2, QUARTER)
+                gather_words(half_words[g, 0][:, QUARTER * quarter : QUARTER * (quarter + 1)], g, quarter, QUARTER)
 
         pairs, grouped = {}, {}
 
@@ -209,13 +209,51 @@ def tile_list_rvq_relu_res_kernel(
 
         def weave(quarter, b):
             half, c0 = divmod(quarter * QUARTER, HALF)
-            if c0 == 0:
+            if (half, b) not in grouped:
                 grouped[half, b] = keep.tile([P, 2 * HALF], F32, name="grouped%d_%d" % (half, b), align_bytes=64)
-            copy = nc.vector.tensor_copy if quarter == 2 else nc.scalar.copy
-            copy(
-                out=grouped[half, b][:, 2 * c0 : 2 * (c0 + QUARTER)].rearrange("p (c i u) -> p c u i", i=4, u=2),
+            woven = grouped[half, b][:, 2 * c0 : 2 * (c0 + QUARTER)]
+            if quarter != 2:
+                nc.gpsimd.tensor_copy(
+                    out=woven.rearrange("p (c u) -> p c u", u=2),
+                    in_=pairs[quarter, b][:].rearrange("p u c -> p c u"),
+                )
+                return
+            nc.vector.tensor_copy(
+                out=woven.rearrange("p (c i u) -> p c u i", i=4, u=2),
                 in_=pairs[quarter, b][:].rearrange("p u (c i) -> p c u i", i=4),
             )
+
+        def wide_pass(acc, half, b, t, g, words, cols, start, stop):
+            s0 = 512 * g + P * t
+            nc.tensor.matmul_mx(
+                out=acc[:, cols],
+                lhsT=w_dealt[g, b][:, 2 * P * t : 2 * P * (t + 1)].bitcast(FP4X4),
+                lhsT_scale=w_scales[b].bitcast(U8)[:, s0 : s0 + P],
+                rhs=words.bitcast(FP8X4),
+                rhs_scale=v_scales[g, half][:, cols],
+                start=start,
+                stop=stop,
+            )
+
+        def wide_out(accs, half, b):
+            wide_pairs = keep.tile([P, 2, HALF], F32, name="wide_pairs%d" % half, align_bytes=64)
+            for t, acc in enumerate(accs):
+                u, e = divmod(t, 2)
+                nc.scalar.activation(
+                    out=wide_pairs[:, u, :].bitcast(BF16).rearrange("p (c e) -> p c e", e=2)[:, :, e],
+                    in_=acc[:],
+                    func=RELU,
+                )
+            return wide_pairs
+
+        def wide_weave(wide_pairs, half, b):
+            if (half, b) not in grouped:
+                grouped[half, b] = keep.tile([P, 2 * HALF], F32, name="grouped%d_%d" % (half, b), align_bytes=64)
+            for c0 in range(0, HALF, QUARTER):
+                nc.gpsimd.tensor_copy(
+                    out=grouped[half, b][:, 2 * c0 : 2 * (c0 + QUARTER)].rearrange("p (c u) -> p c u", u=2),
+                    in_=wide_pairs[:, :, c0 : c0 + QUARTER].rearrange("p u c -> p c u"),
+                )
 
         def group_by_list(units, first_bank):
             keys = [(quarter, b, u) for quarter, b in units for u in range(2)]
@@ -236,54 +274,29 @@ def tile_list_rvq_relu_res_kernel(
                 relu_out(acc, quarter, b, u)
             weave(quarter, b)
 
-        def narrow_unit(first, b, index):
+        def pair_unit(first, width, b, u, index):
             quarter, c0 = divmod(first, QUARTER)
             half, h0 = divmod(first, HALF)
-            acc = bank(index)
-            for t in range(4):
+            acc = bank(index)[:, : 2 * width]
+            for e in range(2):
+                t = 2 * u + e
                 for g in range(LISTS):
                     s0 = 512 * g + P * t
                     nc.tensor.matmul_mx(
-                        out=acc[:, P * t : P * (t + 1)],
+                        out=acc[:, width * e : width * (e + 1)],
                         lhsT=w_dealt[g, b][:, 2 * P * t : 2 * P * (t + 1)].bitcast(FP4X4),
                         lhsT_scale=w_scales[b].bitcast(U8)[:, s0 : s0 + P],
-                        rhs=v_words[g, quarter][:, c0 : c0 + P].bitcast(FP8X4),
-                        rhs_scale=v_scales[g, half][:, h0 : h0 + P],
+                        rhs=v_words[g, quarter][:, c0 : c0 + width].bitcast(FP8X4),
+                        rhs_scale=v_scales[g, half][:, h0 : h0 + width],
                         start=(g == 0),
                         stop=(g == LISTS - 1),
                     )
+            woven = grouped[half, b][:, 2 * h0 : 2 * (h0 + width)].bitcast(BF16)
             nc.scalar.activation(
-                out=grouped[half, b][:, 2 * h0 : 2 * (h0 + P)].bitcast(BF16).rearrange(
-                    "p (c i t) -> p c t i", i=2, t=4
-                ),
-                in_=acc[:].rearrange("p (t c i) -> p c t i", i=2, t=4),
+                out=woven.rearrange("p (c i t) -> p c t i", i=2, t=4)[:, :, 2 * u : 2 * u + 2, :],
+                in_=acc.rearrange("p (t c i) -> p c t i", i=2, t=2),
                 func=RELU,
             )
-
-        def last_unit(first, b, banks):
-            quarter, c0 = divmod(first, QUARTER)
-            half, h0 = divmod(first, HALF)
-            woven = grouped[half, b][:, 2 * h0 : 2 * (h0 + P)].bitcast(BF16).rearrange("p (c i t) -> p c t i", i=2, t=4)
-            for u, index in enumerate(banks):
-                acc = bank(index)[:, : 2 * P]
-                for e in range(2):
-                    t = 2 * u + e
-                    for g in range(LISTS):
-                        s0 = 512 * g + P * t
-                        nc.tensor.matmul_mx(
-                            out=acc[:, P * e : P * (e + 1)],
-                            lhsT=w_dealt[g, b][:, 2 * P * t : 2 * P * (t + 1)].bitcast(FP4X4),
-                            lhsT_scale=w_scales[b].bitcast(U8)[:, s0 : s0 + P],
-                            rhs=v_words[g, quarter][:, c0 : c0 + P].bitcast(FP8X4),
-                            rhs_scale=v_scales[g, half][:, h0 : h0 + P],
-                            start=(g == 0),
-                            stop=(g == LISTS - 1),
-                        )
-                nc.scalar.activation(
-                    out=woven[:, :, 2 * u : 2 * u + 2, :],
-                    in_=acc.rearrange("p (t c i) -> p c t i", i=2, t=2),
-                    func=RELU,
-                )
 
         h_codes, h_scales = {}, {}
 
@@ -324,10 +337,6 @@ def tile_list_rvq_relu_res_kernel(
             nc.vector.tensor_tensor(out=out_sb[:, m, cols], in0=acc, in1=res_sb[:, m, cols], op=ADD)
             store(first, width, slice(m, m + 1))
 
-        def second_layer_wide(first, first_bank):
-            for m in range(N_TILES):
-                second_layer_tile(first, HALF, m, first_bank + m)
-
         def narrow_bank(index):
             return bank(index)[:, : N_TILES * P].rearrange("p (m j) -> p m j", m=N_TILES)
 
@@ -339,25 +348,36 @@ def tile_list_rvq_relu_res_kernel(
             cols = slice(first, first + P)
             nc.vector.tensor_tensor(out=out_sb[:, :, cols], in0=acc, in1=res_sb[:, :, cols], op=ADD)
 
-        group_by_list([(0, 0), (1, 0)], 0)
-        group_by_list([(0, 1), (1, 1)], 4)
         for g in range(LISTS):
-            gather_scales(g, 1)
-        last_words = words_tile("v_words2_1", LISTS * QUARTER)
+            gather_words(words_tile("third_words%d" % g, QUARTER)[:], g, 2, QUARTER)
+        group_by_list([(0, 0), (1, 0)], 0)
+        accs = [bank(4 + t) for t in range(4)]
+        for t in range(4):
+            wide_pass(accs[t], 0, 1, t, 0, half_words[0, 0][:], slice(0, HALF), True, False)
+        gather_scales(0, 1, "v_scales0")
+        gather_scales(1, 1, "v_words0")
+        for t in range(4):
+            for g in range(1, LISTS):
+                wide_pass(accs[t], 0, 1, t, g, half_words[g, 0][:], slice(0, HALF), False, g == LISTS - 1)
+        gather_scales(2, 1, "v_scales2")
+        wide_weave(wide_out(accs, 0, 1), 0, 1)
+        last_words = words_tile("v_words2", LISTS * QUARTER)
         for g in range(LISTS):
             gather_words(last_words[:, QUARTER * g : QUARTER * (g + 1)], g, 3, QUARTER)
         group_by_list([(2, 0), (2, 1)], 0)
-        quantise(0, HALF, 0, tag="v_words0_2")
-        quantise(0, HALF, 1, tag="v_words1_2")
+        quantise(0, HALF, 0, tag="third_words0")
+        quantise(0, HALF, 1, tag="third_words1")
         quantise(2 * QUARTER, QUARTER, 0)
         quantise(2 * QUARTER, QUARTER, 1)
         unit_by_bank(3, 0, 4)
-        second_layer_wide(0, 6)
+        second_layer_tile(0, HALF, 0, 6)
+        pair_unit(3 * QUARTER, QUARTER, 1, 0, 0)
+        second_layer_tile(0, HALF, 1, 7)
         quantise(3 * QUARTER, QUARTER, 0)
-        narrow_unit(3 * QUARTER, 1, 0)
+        pair_unit(3 * QUARTER, P, 1, 1, 1)
         quantise(3 * QUARTER, P, 1)
-        last_unit(3 * QUARTER + P, 1, (1, 6))
-        second_layer_tile(2 * QUARTER, QUARTER, 0, 2)
+        pair_unit(3 * QUARTER + P, P, 1, 1, 2)
+        second_layer_tile(2 * QUARTER, QUARTER, 0, 6)
         quantise(3 * QUARTER + P, P, 1)
         second_layer_tile(2 * QUARTER, QUARTER, 1, 3)
         before_last, last = narrow_bank(4), narrow_bank(5)

@@ -212,48 +212,17 @@ def tile_list_rvq_relu_res_kernel(
             if (half, b) not in grouped:
                 grouped[half, b] = keep.tile([P, 2 * HALF], F32, name="grouped%d_%d" % (half, b), align_bytes=64)
             woven = grouped[half, b][:, 2 * c0 : 2 * (c0 + QUARTER)]
-            if quarter != 2:
+            if b == 0 and quarter != 2:
                 nc.gpsimd.tensor_copy(
                     out=woven.rearrange("p (c u) -> p c u", u=2),
                     in_=pairs[quarter, b][:].rearrange("p u c -> p c u"),
                 )
                 return
-            nc.vector.tensor_copy(
+            copy = nc.vector.tensor_copy if quarter == 2 else nc.scalar.copy
+            copy(
                 out=woven.rearrange("p (c i u) -> p c u i", i=4, u=2),
                 in_=pairs[quarter, b][:].rearrange("p u (c i) -> p c u i", i=4),
             )
-
-        def wide_pass(acc, half, b, t, g, words, cols, start, stop):
-            s0 = 512 * g + P * t
-            nc.tensor.matmul_mx(
-                out=acc[:, cols],
-                lhsT=w_dealt[g, b][:, 2 * P * t : 2 * P * (t + 1)].bitcast(FP4X4),
-                lhsT_scale=w_scales[b].bitcast(U8)[:, s0 : s0 + P],
-                rhs=words.bitcast(FP8X4),
-                rhs_scale=v_scales[g, half][:, cols],
-                start=start,
-                stop=stop,
-            )
-
-        def wide_out(accs, half, b):
-            wide_pairs = keep.tile([P, 2, HALF], F32, name="wide_pairs%d" % half, align_bytes=64)
-            for t, acc in enumerate(accs):
-                u, e = divmod(t, 2)
-                nc.scalar.activation(
-                    out=wide_pairs[:, u, :].bitcast(BF16).rearrange("p (c e) -> p c e", e=2)[:, :, e],
-                    in_=acc[:],
-                    func=RELU,
-                )
-            return wide_pairs
-
-        def wide_weave(wide_pairs, half, b):
-            if (half, b) not in grouped:
-                grouped[half, b] = keep.tile([P, 2 * HALF], F32, name="grouped%d_%d" % (half, b), align_bytes=64)
-            for c0 in range(0, HALF, QUARTER):
-                nc.gpsimd.tensor_copy(
-                    out=grouped[half, b][:, 2 * c0 : 2 * (c0 + QUARTER)].rearrange("p (c u) -> p c u", u=2),
-                    in_=wide_pairs[:, :, c0 : c0 + QUARTER].rearrange("p u c -> p c u"),
-                )
 
         def group_by_list(units, first_bank):
             keys = [(quarter, b, u) for quarter, b in units for u in range(2)]
@@ -351,16 +320,9 @@ def tile_list_rvq_relu_res_kernel(
         for g in range(LISTS):
             gather_words(words_tile("third_words%d" % g, QUARTER)[:], g, 2, QUARTER)
         group_by_list([(0, 0), (1, 0)], 0)
-        accs = [bank(4 + t) for t in range(4)]
-        for t in range(4):
-            wide_pass(accs[t], 0, 1, t, 0, half_words[0, 0][:], slice(0, HALF), True, False)
-        gather_scales(0, 1, "v_scales0")
-        gather_scales(1, 1, "v_words0")
-        for t in range(4):
-            for g in range(1, LISTS):
-                wide_pass(accs[t], 0, 1, t, g, half_words[g, 0][:], slice(0, HALF), False, g == LISTS - 1)
-        gather_scales(2, 1, "v_scales2")
-        wide_weave(wide_out(accs, 0, 1), 0, 1)
+        group_by_list([(0, 1), (1, 1)], 4)
+        for g in range(LISTS):
+            gather_scales(g, 1, "v_scales%d" % g)
         last_words = words_tile("v_words2", LISTS * QUARTER)
         for g in range(LISTS):
             gather_words(last_words[:, QUARTER * g : QUARTER * (g + 1)], g, 3, QUARTER)

from contextlib import ExitStack
from itertools import product

import concourse.mybir as mybir

K, R, N, T, J = 512, 1024, 256, 4096, 1024
FLOPS = 2 * (3 * K * R * J + R * N * J)

F32 = mybir.dt.float32
BF16 = mybir.dt.bfloat16
I32 = mybir.dt.int32
U32 = mybir.dt.uint32
U16 = mybir.dt.uint16
U8 = mybir.dt.uint8
FP8X4 = mybir.dt.float8_e4m3fn_x4
FP4X4 = mybir.dt.float4_e2m1fn_x4
RELU = mybir.ActivationFunctionType.Relu
ADD = mybir.AluOpType.add

P = 128
LISTS = 3
HALF = 512
QUARTER = 256
BANK = 512
R_PASSES = R // 512
N_TILES = N // P
WARM_PASSES = 5
TABLE_HEAD = 448
TABLE_TAIL = 2304


def tile_list_rvq_relu_res_kernel(
    tc, tab_words, tab_scales, w0_words, w0_scales, w1_words, w1_scales, w2_words, w2_scales,
    wd_words, wd_scales, res, offs, out,
):
    nc = tc.nc
    w_words_hbm = [w0_words, w1_words, w2_words]
    w_scales_hbm = [w0_scales, w1_scales, w2_scales]

    with ExitStack() as ctx:
        keep = ctx.enter_context(tc.tile_pool(name="keep", bufs=1))
        psum = ctx.enter_context(tc.psum_pool(name="psum", bufs=1))

        def bank(index):
            return psum.tile([P, BANK], F32, name="bank%d" % index)

        offsets = keep.tile([P, LISTS * J // 16], U16, name="offsets")
        table = keep.tile([P, T], I32, name="table", align_bytes=64)
        table_scales = keep.tile([P, T // 4], I32, name="table_scales", align_bytes=64)
        staged_tile = keep.tile([P, LISTS * P], I32, name="staged", align_bytes=64)
        high = keep.tile([P, (LISTS + 1) * P], I32, name="w_scales_high", align_bytes=256)
        low = keep.tile([P, (LISTS + 1) * P], I32, name="w_scales_low", align_bytes=256)
        staged = staged_tile[:]
        w_scales = [low[:, : LISTS * P], high[:, : LISTS * P]]
        wd_staged, wd_sc = low[:, LISTS * P :], high[:, LISTS * P :].bitcast(U8)
        wd = keep.tile([P, R_PASSES, N], I32, name="wd", align_bytes=256)
        res_sb = keep.tile([P, N_TILES, J], F32, name="res_sb")
        out_sb = keep.tile([P, N_TILES, J], F32, name="out_sb")

        warm = keep.tile([P, 64 + BANK + BANK // 4], I32, name="warm", align_bytes=64)
        for g in range(LISTS):
            nc.gpsimd.memset(staged[:, P * g : P * (g + 1)], 0)
        nc.vector.memset(table_scales[:], 0)
        nc.vector.memset(warm[:], 0)
        nc.vector.memset(high[:], 0)
        nc.gpsimd.memset(wd_staged, 0)

        table_hbm = tab_words[0].rearrange("p t i -> p (t i)").bitcast(I32)
        nc.sync.dma_start(offsets[:], offs)
        for g in range(LISTS):
            if g == 1:
                nc.sync.dma_start(out=table[:, :TABLE_HEAD], in_=table_hbm[:, :TABLE_HEAD])
            nc.sync.dma_start(
                out=staged[0:P:4, P * g : P * (g + 1)],
                in_=w_scales_hbm[g][0].bitcast(I32).rearrange("q (b c) -> (q b) c", b=R_PASSES),
            )
        for g in range(LISTS):
            cols = slice(512 * g, 512 * (g + 1))
            engine = nc.gpsimd if g < LISTS - 1 else nc.vector
            engine.tensor_copy(
                out=w_scales[0].bitcast(U8)[:, cols].rearrange("p (t c i) -> p c t i", t=4, i=16),
                in_=staged.bitcast(U8)[:, cols].rearrange("p (c i t) -> p c t i", t=4, i=16),
            )

        def load_scale_rows(plane, rows):
            for r in range(4):
                nc.sync.dma_start(out=plane[r:P:32], in_=rows[r:16:4])

        def carry_low_rows():
            for r in range(1, 4):
                nc.sync.dma_start(out=w_scales[0][r:P:32, :], in_=w_scales[0][8 * r : P : 32, :])

        def carry_high_rows():
            for r in range(4):
                nc.sync.dma_start(out=high[r:P:32, :], in_=low[8 * r + 4 : P : 32, :])

        def warm_up():
            zeros = warm[:, :64].bitcast(BF16)
            zero_codes = warm[:, 64 : 64 + BANK]
            zero_scales = warm[:, 64 + BANK :].bitcast(U8)
            nc.vector.quantize_mx(out=zero_codes[:, :32].bitcast(FP8X4), scales=zero_scales[:, :32], in_=zeros)
            warm_bank = bank(0)
            for warm_pass in range(WARM_PASSES):
                nc.tensor.matmul_mx(
                    out=warm_bank[:],
                    lhsT=zero_codes[:, :P].bitcast(FP8X4),
                    lhsT_scale=(zero_scales if warm_pass else wd_staged.bitcast(U8))[:, :P],
                    rhs=zero_codes.bitcast(FP8X4),
                    rhs_scale=zero_scales,
                    start=True,
                    stop=True,
                )

        w_raw = {}

        def load_weight(g, passes):
            raw = keep.tile([P, 256 * len(passes)], I32, name="w_raw%d_%d" % (g, passes[0]), align_bytes=256)
            nc.sync.dma_start(
                out=raw[:], in_=w_words_hbm[g][0].bitcast(I32)[:, 256 * passes[0] : 256 * (passes[-1] + 1)]
            )
            for place, b in enumerate(passes):
                w_raw[g, b] = raw[:, 256 * place : 256 * (place + 1)]

        load_scale_rows(table_scales, tab_scales[0].bitcast(I32))
        nc.sync.dma_start(out=table[:, TABLE_HEAD:TABLE_TAIL], in_=table_hbm[:, TABLE_HEAD:TABLE_TAIL])
        nc.sync.dma_start(
            out=wd_staged[4:P:8].rearrange("q (a n) -> q a n", a=R_PASSES),
            in_=wd_scales.bitcast(I32).rearrange("a q n -> q a n"),
        )
        nc.sync.dma_start(out=table[:, TABLE_TAIL:], in_=table_hbm[:, TABLE_TAIL:])
        warm_up()
        load_weight(0, (0,))
        carry_low_rows()
        load_weight(1, (0,))
        load_weight(2, (0, 1))
        load_weight(0, (1,))
        load_weight(1, (1,))
        carry_high_rows()
        nc.sync.dma_start(
            out=wd[:], in_=wd_words.rearrange("a p n i -> p a (n i)").bitcast(I32)
        )
        nc.sync.dma_start(out=res_sb[:], in_=res.rearrange("(m p) j -> p m j", p=P))

        w_dealt = {}
        for b, g in product(range(R_PASSES), range(LISTS)):
            dealt = keep.tile([P, 1024], U8, name="w_dealt%d_%d" % (g, b), align_bytes=256)
            parts = (slice(0, 2), slice(2, 4)) if (g, b) == (0, 0) else (slice(0, 4),)
            for part in parts:
                nc.scalar.copy(
                    out=dealt[:].bitcast(U16).rearrange("p (t c i) -> p c t i", t=4, i=8)[:, :, part, :],
                    in_=w_raw[g, b].bitcast(U16).rearrange("p (c i t) -> p c t i", t=4, i=8)[:, :, part, :],
                )
            w_dealt[g, b] = dealt

        v_words, v_scales = {}, {}

        def gather(picked, window, g, first, count):
            column = (g * J + first) // 16
            nc.vector.tensor_copy(picked, window.indirect(offsets[:, column : column + count // 16]))

        def gather_words(picked, g, first_quarter, count):
            gather(picked, table[:].bitcast(U32), g, first_quarter * QUARTER, count)
            for c0 in range(0, count, QUARTER):
                v_words[g, first_quarter + c0 // QUARTER] = picked[:, c0 : c0 + QUARTER]

        def words_tile(name, width):
            return keep.tile([P, width], U32, name=name, align_bytes=256)

        def gather_scales(g, half, place):
            picked = keep.tile([P, HALF], U8, name=place, align_bytes=256)
            gather(picked[:], table_scales[:].bitcast(U8), g, half * HALF, HALF)
            v_scales[g, half] = picked

        half_words = {}
        for g in range(LISTS):
            gather_scales(g, 0, "v_scales%d" % g)
        for g in range(LISTS):
            half_words[g, 0] = words_tile("v_words%d" % g, HALF)
            for quarter in range(2):
                gather_words(half_words[g, 0][:, QUARTER * quarter : QUARTER * (quarter + 1)], g, quarter, QUARTER)

        pairs, grouped = {}, {}

        def first_passes(acc, quarter, b, u, g):
            half, c0 = divmod(quarter * QUARTER, HALF)
            for e in range(2):
                t = 2 * u + e
                s0 = 512 * g + P * t
                nc.tensor.matmul_mx(
                    out=acc[:, QUARTER * e : QUARTER * (e + 1)],
                    lhsT=w_dealt[g, b][:, 2 * P * t : 2 * P * (t + 1)].bitcast(FP4X4),
                    lhsT_scale=w_scales[b].bitcast(U8)[:, s0 : s0 + P],
                    rhs=v_words[g, quarter].bitcast(FP8X4),
                    rhs_scale=v_scales[g, half][:, c0 : c0 + QUARTER],
                    start=(g == 0 and e == 0),
                    stop=(g == LISTS - 1 and e == 1),
                )

        def relu_out(acc, quarter, b, u):
            if u == 0:
                pairs[quarter, b] = keep.tile(
                    [P, 2, QUARTER], F32, name="pairs%d_%d" % (quarter, b), align_bytes=64
                )
            nc.scalar.activation(
                out=pairs[quarter, b][:, u, :].bitcast(BF16).rearrange("p (c i e) -> p c e i", i=2, e=2),
                in_=acc[:].rearrange("p (e c i) -> p c e i", i=2, e=2),
                func=RELU,
            )

        def weave(quarter, b):
            half, c0 = divmod(quarter * QUARTER, HALF)
            if (half, b) not in grouped:
                grouped[half, b] = keep.tile([P, 2 * HALF], F32, name="grouped%d_%d" % (half, b), align_bytes=64)
            woven = grouped[half, b][:, 2 * c0 : 2 * (c0 + QUARTER)]
            if b == 0 and quarter != 2:
                nc.gpsimd.tensor_copy(
                    out=woven.rearrange("p (c u) -> p c u", u=2),
                    in_=pairs[quarter, b][:].rearrange("p u c -> p c u"),
                )
                return
            copy = nc.vector.tensor_copy if quarter == 2 else nc.scalar.copy
            copy(
                out=woven.rearrange("p (c i u) -> p c u i", i=4, u=2),
                in_=pairs[quarter, b][:].rearrange("p u (c i) -> p c u i", i=4),
            )

        def group_by_list(units, first_bank):
            keys = [(quarter, b, u) for quarter, b in units for u in range(2)]
            accs = [bank(first_bank + place) for place in range(len(keys))]
            for g in range(LISTS):
                for acc, (quarter, b, u) in zip(accs, keys):
                    first_passes(acc, quarter, b, u, g)
                    if g == LISTS - 1:
                        relu_out(acc, quarter, b, u)
            for quarter, b in units:
                weave(quarter, b)

        def unit_by_bank(quarter, b, first_bank):
            for u in range(2):
                acc = bank(first_bank + u)
                for g in range(LISTS):
                    first_passes(acc, quarter, b, u, g)
                relu_out(acc, quarter, b, u)
            weave(quarter, b)

        def pair_unit(first, width, b, u, index):
            quarter, c0 = divmod(first, QUARTER)
            half, h0 = divmod(first, HALF)
            acc = bank(index)[:, : 2 * width]
            for e in range(2):
                t = 2 * u + e
                for g in range(LISTS):
                    s0 = 512 * g + P * t
                    nc.tensor.matmul_mx(
                        out=acc[:, width * e : width * (e + 1)],
                        lhsT=w_dealt[g, b][:, 2 * P * t : 2 * P * (t + 1)].bitcast(FP4X4),
                        lhsT_scale=w_scales[b].bitcast(U8)[:, s0 : s0 + P],
                        rhs=v_words[g, quarter][:, c0 : c0 + width].bitcast(FP8X4),
                        rhs_scale=v_scales[g, half][:, h0 : h0 + width],
                        start=(g == 0),
                        stop=(g == LISTS - 1),
                    )
            woven = grouped[half, b][:, 2 * h0 : 2 * (h0 + width)].bitcast(BF16)
            nc.scalar.activation(
                out=woven.rearrange("p (c i t) -> p c t i", i=2, t=4)[:, :, 2 * u : 2 * u + 2, :],
                in_=acc.rearrange("p (t c i) -> p c t i", i=2, t=2),
                func=RELU,
            )

        h_codes, h_scales = {}, {}

        def quantise(first, width, b, tag=None):
            half, c0 = divmod(first, HALF)
            codes = keep.tile([P, width], U32, name=tag or "h_codes%d_%d" % (first, b), align_bytes=256)
            scales = keep.tile([P, width], U8, name="h_scales%d_%d" % (first, b), align_bytes=256)
            nc.vector.quantize_mx(
                out=codes[:].bitcast(FP8X4),
                scales=scales[:],
                in_=grouped[half, b][:, 2 * c0 : 2 * (c0 + width)].bitcast(BF16),
            )
            for c in range(0, width, P):
                h_codes[first + c, b], h_scales[first + c, b] = (codes, c), (scales, c)

        def second_pass(acc, first, width, b, m, start, stop):
            codes, c0 = h_codes[first, b]
            scales, c0 = h_scales[first, b]
            nc.tensor.matmul_mx(
                out=acc,
                lhsT=wd[:, b, P * m : P * (m + 1)].bitcast(FP8X4),
                lhsT_scale=wd_sc[:, N * b + P * m : N * b + P * (m + 1)],
                rhs=codes[:, c0 : c0 + width].bitcast(FP8X4),
                rhs_scale=scales[:, c0 : c0 + width],
                start=start,
                stop=stop,
            )

        def store(first, width, rows=slice(0, N_TILES)):
            cols = slice(first, first + width)
            nc.sync.dma_start(out=out.rearrange("(m p) j -> p m j", p=P)[:, rows, cols], in_=out_sb[:, rows, cols])

        def second_layer_tile(first, width, m, index):
            cols = slice(first, first + width)
            acc = bank(index)[:, :width]
            for b in range(R_PASSES):
                second_pass(acc, first, width, b, m, b == 0, b == R_PASSES - 1)
            nc.vector.tensor_tensor(out=out_sb[:, m, cols], in0=acc, in1=res_sb[:, m, cols], op=ADD)
            store(first, width, slice(m, m + 1))

        def narrow_bank(index):
            return bank(index)[:, : N_TILES * P].rearrange("p (m j) -> p m j", m=N_TILES)

        def narrow_passes(acc, first, b):
            for m in range(N_TILES):
                second_pass(acc[:, m, :], first, P, b, m, b == 0 and m == 0, b == R_PASSES - 1 and m == N_TILES - 1)

        def narrow_out(acc, first):
            cols = slice(first, first + P)
            nc.vector.tensor_tensor(out=out_sb[:, :, cols], in0=acc, in1=res_sb[:, :, cols], op=ADD)

        for g in range(LISTS):
            gather_words(words_tile("third_words%d" % g, QUARTER)[:], g, 2, QUARTER)
        group_by_list([(0, 0), (1, 0)], 0)
        group_by_list([(0, 1), (1, 1)], 4)
        for g in range(LISTS):
            gather_scales(g, 1, "v_scales%d" % g)
        last_words = words_tile("v_words2", LISTS * QUARTER)
        for g in range(LISTS):
            gather_words(last_words[:, QUARTER * g : QUARTER * (g + 1)], g, 3, QUARTER)
        group_by_list([(2, 0), (2, 1)], 0)
        quantise(0, HALF, 0, tag="third_words0")
        quantise(0, HALF, 1, tag="third_words1")
        quantise(2 * QUARTER, QUARTER, 0)
        quantise(2 * QUARTER, QUARTER, 1)
        unit_by_bank(3, 0, 4)
        second_layer_tile(0, HALF, 0, 6)
        pair_unit(3 * QUARTER, QUARTER, 1, 0, 0)
        second_layer_tile(0, HALF, 1, 7)
        quantise(3 * QUARTER, QUARTER, 0)
        pair_unit(3 * QUARTER, P, 1, 1, 1)
        quantise(3 * QUARTER, P, 1)
        pair_unit(3 * QUARTER + P, P, 1, 1, 2)
        second_layer_tile(2 * QUARTER, QUARTER, 0, 6)
        quantise(3 * QUARTER + P, P, 1)
        second_layer_tile(2 * QUARTER, QUARTER, 1, 3)
        before_last, last = narrow_bank(4), narrow_bank(5)
        for b in range(R_PASSES):
            narrow_passes(before_last, 3 * QUARTER, b)
        narrow_out(before_last, 3 * QUARTER)
        store(3 * QUARTER, P)
        for b in range(R_PASSES):
            narrow_passes(last, 3 * QUARTER + P, b)
        narrow_out(last, 3 * QUARTER + P)
        store(3 * QUARTER + P, P)
